import numpy as np
import ml_dtypes


def mxq(x, axis, fmt="e4m3"):
    dtype, down = {"e4m3": (ml_dtypes.float8_e4m3fn, 7), "e5m2": (ml_dtypes.float8_e5m2, 14)}[fmt]
    v = np.moveaxis(np.asarray(x, np.float32).astype(ml_dtypes.bfloat16).astype(np.float64), axis, -1)
    blocks = v.reshape(v.shape[:-1] + (-1, 32))
    amax = np.abs(blocks).max(-1, keepdims=True)
    byte = np.maximum(np.where(amax > 0, np.frexp(amax)[1] - 1 + 127, 0) - down, 1)
    scale = np.exp2(byte - 127.0)
    codes = (blocks / scale).astype(np.float32).astype(dtype).astype(np.float64)
    return np.moveaxis((codes * scale).reshape(v.shape), -1, axis)


WIDE = False


def mx_kscale(k):
    if not WIDE:
        return np.ones(k)
    levels = np.array([10, -10, 5, -5, 0])
    if k % 512:
        return np.exp2(np.random.permutation(np.resize(levels, k // 32))).repeat(32)
    a = np.empty((k // 512, 16))
    for p in range(k // 512):
        a[p, :8] = np.random.permutation(np.resize(levels, 8))
        for g in range(8):
            far = levels[np.abs(levels - a[p, g]) >= 10]
            a[p, g + 8] = far[np.random.randint(len(far))]
    return np.exp2(a.ravel()).repeat(32)


def f64(x):
    return np.asarray(x).astype(np.float64)


def striped(idx):
    return np.tile(np.asarray(idx).reshape(-1, 16).T, (8, 1)).astype(np.uint16)


def unstriped(offs):
    return offs[:16].T.reshape(-1).astype(np.int64)


E2M1 = np.array([0.0, 0.5, 1.0, 1.5, 2.0, 3.0, 4.0, 6.0, -0.0, -0.5, -1.0, -1.5, -2.0, -3.0, -4.0, -6.0])


def pack_weight(w, fmt):
    k, n = w.shape
    w = f64(np.asarray(w, np.float32).astype(ml_dtypes.bfloat16)).reshape(k // 32, 32, n)
    amax = np.abs(w).max(1)
    if fmt == "e4m3":
        byte = np.frexp(amax)[1] - 1 + 127 - 7
    else:
        mant, ex = np.frexp(amax / 6.0)
        byte = np.where(mant > 0.5, ex, ex - 1) + 127
    byte = np.clip(np.where(amax > 0, byte, 1), 1, 254)
    scaled = (w * np.exp2(127.0 - byte)[:, None, :]).reshape(k, n).astype(np.float32)
    by_word = np.ascontiguousarray(scaled.reshape(k // 512, 128, 4, n).transpose(0, 1, 3, 2))
    if fmt == "e4m3":
        words = by_word.astype(ml_dtypes.float8_e4m3fn).view(np.uint8)
    else:
        c = by_word.astype(ml_dtypes.float4_e2m1fn).view(np.uint8) & 0xF
        words = (c[..., 0::2] | (c[..., 1::2] << 4)).reshape(k // 512, 128, 2 * n)
    return np.ascontiguousarray(words), np.ascontiguousarray(byte.astype(np.uint8).reshape(k // 512, 16, n))


def unpack_weight(words, scales, fmt):
    g, _, n = scales.shape
    words = np.ascontiguousarray(words).reshape(g, 128, n, -1)
    if fmt == "e4m3":
        vals = words.view(ml_dtypes.float8_e4m3fn).astype(np.float64)
    else:
        nib = np.empty((g, 128, n, 4), np.uint8)
        nib[..., 0::2] = words & 0xF
        nib[..., 1::2] = words >> 4
        vals = E2M1[nib]
    vals = vals * np.repeat(np.exp2(scales.astype(np.float64) - 127.0), 8, axis=1)[..., None]
    return vals.transpose(0, 1, 3, 2).reshape(g * 512, n)


B, N, T, D, NQ = 1, 512, 2048, 512, 128


def setup_inputs():
    n = np.random.standard_normal
    idx = np.random.permutation(T)[:B * N]
    s = mx_kscale(D)[:, None]
    kp = pack_weight(n((D, T)) / s, "e4m3")
    return {
        "qT": (n((B, D, NQ)) * s * (1.00 / np.sqrt(D))).astype(np.float32),
        "k_words": kp[0],
        "k_scales": kp[1],
        "nb": np.tile(0.5 * n(2048), (128, 1)).astype(np.float32),
        "offs": striped(idx),
    }


def reference(qT, k_words, k_scales, nb, offs):
    idx = unstriped(offs)
    pick = lambda x, which: x[:, which].reshape(x.shape[0], B, -1).transpose(1, 0, 2)
    k = unpack_weight(k_words, k_scales, "e4m3")
    kg = pick(k, idx)
    qq = mxq(f64(qT), 1, "e4m3")
    a = qq.transpose(0, 2, 1) @ kg
    y = np.maximum(a + pick(f64(nb), idx)[:, :1, :], 0.0)
    out = np.zeros((B, NQ, T))
    for b in range(B):
        out[b][:, idx[b * N:(b + 1) * N]] = y[b]
    return out

@@ -1,0 +1,108 @@
+from contextlib import ExitStack
+
+import concourse.mybir as mybir
+from concourse.masks import make_identity
+
+P = 128
+T = 2048
+N = 512
+D = 512
+NQ = 128
+PACK = 4
+HALF = N // 2
+
+FLOPS = 2 * D * NQ * N
+
+F32 = mybir.dt.float32
+BF16 = mybir.dt.bfloat16
+I32 = mybir.dt.int32
+U32 = mybir.dt.uint32
+U16 = mybir.dt.uint16
+U8 = mybir.dt.uint8
+FP8X4 = mybir.dt.float8_e4m3fn_x4
+ACT = mybir.ActivationFunctionType
+ALU = mybir.AluOpType
+
+
+def tile_attend_neu_scat_topk_kernel(tc, qT, k_words, k_scales, nb, offs, out):
+    nc = tc.nc
+    with ExitStack() as ctx:
+        sb = ctx.enter_context(tc.tile_pool(name="sb", bufs=1))
+        ps = ctx.enter_context(tc.psum_pool(name="ps", bufs=1))
+
+        offsets = sb.tile([P, N // 16], U16, name="offsets")
+        q_raw = sb.tile([P, PACK, NQ], F32, name="q_raw")
+        scale_win = sb.tile([P, T], U8, name="scale_win", align_bytes=64)
+        word_win = sb.tile([P, T], U32, name="word_win", align_bytes=64)
+        nb_win = sb.tile([P, T], F32, name="nb_win")
+        out_win = sb.tile([P, T], F32, name="out_win")
+        ident = sb.tile([P, P], F32, name="ident")
+
+        def half_list(h):
+            return offsets[:, h * (HALF // 16) : (h + 1) * (HALF // 16)]
+
+        nc.vector.memset(scale_win[:].bitcast(I32), 0)
+        nc.vector.memset(nb_win[:], 0.0)
+        nc.vector.memset(out_win[:], 0.0)
+        make_identity(nc, ident[:])
+
+        nc.sync.dma_start(offsets[:], offs)
+        nc.sync.dma_start(q_raw[:], qT[0].rearrange("(p j) w -> p j w", j=PACK))
+        for r in range(4):
+            nc.sync.dma_start(scale_win[r:P:32, :].bitcast(I32), k_scales[0, r:16:4, :].bitcast(I32))
+        nc.sync.dma_start(word_win[:].bitcast(I32), k_words[0].rearrange("p n t -> p (n t)").bitcast(I32))
+        nc.scalar.dma_start(nb_win[0:1, :], nb[0:1, :])
+
+        q_bf = sb.tile([P, NQ, PACK], BF16, name="q_bf", align_bytes=64)
+        nc.scalar.activation(q_bf[:], q_raw[:].rearrange("p j w -> p w j"), ACT.Copy)
+
+        k_sc = sb.tile([P, N], U8, name="k_sc", align_bytes=64)
+        nc.vector.tensor_copy(k_sc[:], scale_win[:].indirect(offsets[:]))
+
+        bias = []
+        for h in range(2):
+            nb_row = sb.tile([P, HALF], F32, name=f"nb_row{h}")
+            nc.vector.tensor_copy(nb_row[:], nb_win[:].indirect(half_list(h)))
+            turned = ps.tile([P, 2, P], F32, name=f"turned{h}")
+            for c in range(2):
+                nc.tensor.transpose(turned[:, c, :], nb_row[:, c * P : (c + 1) * P], ident[:])
+            nb_col = sb.tile([P, 2], F32, name=f"nb_col{h}")
+            nc.scalar.copy(nb_col[:], turned[:, :, 0])
+            spread = ps.tile([P, 2, P], F32, name=f"spread{h}")
+            for c in range(2):
+                nc.tensor.transpose(spread[:, c, :], nb_col[:, c : c + 1].to_broadcast([P, P]), ident[:])
+            b = sb.tile([P, HALF], F32, name=f"bias{h}")
+            nc.scalar.copy(b[:], spread[:].rearrange("p c s -> p (c s)"))
+            bias.append(b)
+
+        q_codes = sb.tile([P, NQ], U32, name="q_codes", align_bytes=64)
+        q_sc = sb.tile([P, NQ], U8, name="q_sc", align_bytes=64)
+        nc.vector.quantize_mx(out=q_codes[:].bitcast(FP8X4), scales=q_sc[:], in_=q_bf[:].rearrange("p w j -> p (w j)"))
+
+        acc = []
+        for h in range(2):
+            k_codes = sb.tile([P, HALF], U32, name=f"k_codes{h}", align_bytes=64)
+            nc.vector.tensor_copy(k_codes[:], word_win[:].indirect(half_list(h)))
+            a = ps.tile([P, HALF], F32, name=f"acc{h}")
+            nc.tensor.matmul_mx(
+                out=a[:],
+                lhsT=q_codes[:].bitcast(FP8X4),
+                lhsT_scale=q_sc[:],
+                rhs=k_codes[:].bitcast(FP8X4),
+                rhs_scale=k_sc[:, h * HALF : (h + 1) * HALF],
+                start=True,
+                stop=True,
+            )
+            acc.append(a)
+
+        ys = []
+        for h in range(2):
+            s = sb.tile([P, HALF], F32, name=f"pre{h}")
+            nc.vector.tensor_tensor(s[:], acc[h][:], bias[h][:], ALU.add)
+            y = sb.tile([P, HALF], F32, name=f"y{h}")
+            nc.scalar.activation(y[:], s[:], ACT.Relu)
+            ys.append(y)
+        for h in range(2):
+            nc.vector.tensor_copy(out_win[:].indirect(half_list(h)), ys[h][:])
+
+        nc.sync.dma_start(out[0], out_win[:])

@@ -28,36 +28,37 @@ def tile_attend_neu_scat_topk_kernel(tc, qT, k_words, k_scales, nb, offs, out):
     nc = tc.nc
     with ExitStack() as ctx:
         sb = ctx.enter_context(tc.tile_pool(name="sb", bufs=1))
+        shared = ctx.enter_context(tc.tile_pool(name="shared", bufs=1))
         ps = ctx.enter_context(tc.psum_pool(name="ps", bufs=1))
 
         offsets = sb.tile([P, N // 16], U16, name="offsets")
         q_raw = sb.tile([P, PACK, NQ], F32, name="q_raw")
         scale_win = sb.tile([P, T], U8, name="scale_win", align_bytes=64)
         word_win = sb.tile([P, T], U32, name="word_win", align_bytes=64)
-        nb_win = sb.tile([P, T], F32, name="nb_win")
+        nb_win = shared.tile([P, T], F32, name="nb_win", offset=0, align_bytes=64)
         out_win = sb.tile([P, T], F32, name="out_win")
         ident = sb.tile([P, P], F32, name="ident")
 
         def half_list(h):
             return offsets[:, h * (HALF // 16) : (h + 1) * (HALF // 16)]
 
-        nc.vector.memset(scale_win[:].bitcast(I32), 0)
+        nc.gpsimd.memset(scale_win[:].bitcast(I32), 0)
         nc.vector.memset(nb_win[:], 0.0)
         nc.vector.memset(out_win[:], 0.0)
         make_identity(nc, ident[:])
 
         nc.sync.dma_start(offsets[:], offs)
-        nc.sync.dma_start(q_raw[:], qT[0].rearrange("(p j) w -> p j w", j=PACK))
         for r in range(4):
             nc.sync.dma_start(scale_win[r:P:32, :].bitcast(I32), k_scales[0, r:16:4, :].bitcast(I32))
+        nc.sync.dma_start(q_raw[:], qT[0].rearrange("(p j) w -> p j w", j=PACK))
         nc.sync.dma_start(word_win[:].bitcast(I32), k_words[0].rearrange("p n t -> p (n t)").bitcast(I32))
         nc.scalar.dma_start(nb_win[0:1, :], nb[0:1, :])
 
         q_bf = sb.tile([P, NQ, PACK], BF16, name="q_bf", align_bytes=64)
         nc.scalar.activation(q_bf[:], q_raw[:].rearrange("p j w -> p w j"), ACT.Copy)
 
-        k_sc = sb.tile([P, N], U8, name="k_sc", align_bytes=64)
-        nc.vector.tensor_copy(k_sc[:], scale_win[:].indirect(offsets[:]))
+        k_sc0 = sb.tile([P, HALF], U8, name="k_sc0", align_bytes=64)
+        nc.vector.tensor_copy(k_sc0[:], scale_win[:].indirect(half_list(0)))
 
         bias = []
         for h in range(2):
@@ -75,13 +76,16 @@ def tile_attend_neu_scat_topk_kernel(tc, qT, k_words, k_scales, nb, offs, out):
             nc.scalar.copy(b[:], spread[:].rearrange("p c s -> p (c s)"))
             bias.append(b)
 
-        q_codes = sb.tile([P, NQ], U32, name="q_codes", align_bytes=64)
+        k_sc1 = shared.tile([P, HALF], U8, name="k_sc1", offset=0, align_bytes=64)
+        nc.vector.tensor_copy(k_sc1[:], scale_win[:].indirect(half_list(1)))
+        k_sc = [k_sc0, k_sc1]
+        q_codes = shared.tile([P, NQ], U32, name="q_codes", offset=512, align_bytes=64)
         q_sc = sb.tile([P, NQ], U8, name="q_sc", align_bytes=64)
         nc.vector.quantize_mx(out=q_codes[:].bitcast(FP8X4), scales=q_sc[:], in_=q_bf[:].rearrange("p w j -> p (w j)"))
 
         acc = []
         for h in range(2):
-            k_codes = sb.tile([P, HALF], U32, name=f"k_codes{h}", align_bytes=64)
+            k_codes = shared.tile([P, HALF], U32, name=f"k_codes{h}", offset=1024 * (h + 1), align_bytes=64)
             nc.vector.tensor_copy(k_codes[:], word_win[:].indirect(half_list(h)))
             a = ps.tile([P, HALF], F32, name=f"acc{h}")
             nc.tensor.matmul_mx(
@@ -89,7 +93,7 @@ def tile_attend_neu_scat_topk_kernel(tc, qT, k_words, k_scales, nb, offs, out):
                 lhsT=q_codes[:].bitcast(FP8X4),
                 lhsT_scale=q_sc[:],
                 rhs=k_codes[:].bitcast(FP8X4),
-                rhs_scale=k_sc[:, h * HALF : (h + 1) * HALF],
+                rhs_scale=k_sc[h][:],
                 start=True,
                 stop=True,
             )

@@ -20,7 +20,6 @@ U32 = mybir.dt.uint32
 U16 = mybir.dt.uint16
 U8 = mybir.dt.uint8
 FP8X4 = mybir.dt.float8_e4m3fn_x4
-ACT = mybir.ActivationFunctionType
 ALU = mybir.AluOpType
 
 
@@ -43,19 +42,19 @@ def tile_attend_neu_scat_topk_kernel(tc, qT, k_words, k_scales, nb, offs, out):
             return offsets[:, h * (HALF // 16) : (h + 1) * (HALF // 16)]
 
         nc.gpsimd.memset(scale_win[:].bitcast(I32), 0)
-        nc.vector.memset(nb_win[:], 0.0)
-        nc.vector.memset(out_win[:], 0.0)
+        nc.vector.memset(nb_win[:].bitcast(I32), 0)
+        nc.vector.memset(out_win[:].bitcast(I32), 0)
         make_identity(nc, ident[:])
 
         nc.sync.dma_start(offsets[:], offs)
         for r in range(4):
             nc.sync.dma_start(scale_win[r:P:32, :].bitcast(I32), k_scales[0, r:16:4, :].bitcast(I32))
         nc.sync.dma_start(q_raw[:], qT[0].rearrange("(p j) w -> p j w", j=PACK))
+        nc.sync.dma_start(nb_win[0:1, :], nb[0:1, :])
         nc.sync.dma_start(word_win[:].bitcast(I32), k_words[0].rearrange("p n t -> p (n t)").bitcast(I32))
-        nc.scalar.dma_start(nb_win[0:1, :], nb[0:1, :])
 
         q_bf = sb.tile([P, NQ, PACK], BF16, name="q_bf", align_bytes=64)
-        nc.scalar.activation(q_bf[:], q_raw[:].rearrange("p j w -> p w j"), ACT.Copy)
+        nc.scalar.copy(q_bf[:], q_raw[:].rearrange("p j w -> p w j"))
 
         k_sc0 = sb.tile([P, HALF], U8, name="k_sc0", align_bytes=64)
         nc.vector.tensor_copy(k_sc0[:], scale_win[:].indirect(half_list(0)))
@@ -87,7 +86,7 @@ def tile_attend_neu_scat_topk_kernel(tc, qT, k_words, k_scales, nb, offs, out):
         for h in range(2):
             k_codes = shared.tile([P, HALF], U32, name=f"k_codes{h}", offset=1024 * (h + 1), align_bytes=64)
             nc.vector.tensor_copy(k_codes[:], word_win[:].indirect(half_list(h)))
-            a = ps.tile([P, HALF], F32, name=f"acc{h}")
+            a = ps.tile([P, HALF], F32, name=f"acc{h}", tag=("turned1", "spread0")[h])
             nc.tensor.matmul_mx(
                 out=a[:],
                 lhsT=q_codes[:].bitcast(FP8X4),
@@ -99,14 +98,14 @@ def tile_attend_neu_scat_topk_kernel(tc, qT, k_words, k_scales, nb, offs, out):
             )
             acc.append(a)
 
-        ys = []
+        pre = []
         for h in range(2):
             s = sb.tile([P, HALF], F32, name=f"pre{h}")
             nc.vector.tensor_tensor(s[:], acc[h][:], bias[h][:], ALU.add)
-            y = sb.tile([P, HALF], F32, name=f"y{h}")
-            nc.scalar.activation(y[:], s[:], ACT.Relu)
-            ys.append(y)
+            pre.append(s)
+        y = sb.tile([P, N], F32, name="y")
         for h in range(2):
-            nc.vector.tensor_copy(out_win[:].indirect(half_list(h)), ys[h][:])
+            nc.vector.tensor_scalar_max(y[:, h * HALF : (h + 1) * HALF], pre[h][:], 0.0)
+        nc.vector.tensor_copy(out_win[:].indirect(offsets[:]), y[:])
 
         nc.sync.dma_start(out[0], out_win[:])

@@ -41,15 +41,16 @@ def tile_attend_neu_scat_topk_kernel(tc, qT, k_words, k_scales, nb, offs, out):
         def half_list(h):
             return offsets[:, h * (HALF // 16) : (h + 1) * (HALF // 16)]
 
-        nc.gpsimd.memset(scale_win[:].bitcast(I32), 0)
+        nc.vector.memset(scale_win[:].bitcast(I32), 0)
         nc.vector.memset(nb_win[:].bitcast(I32), 0)
+        nc.vector.memset(ident[:], 0.0)
         nc.vector.memset(out_win[:].bitcast(I32), 0)
-        make_identity(nc, ident[:])
+        make_identity(nc, ident[:], nomemset=True)
 
         nc.sync.dma_start(offsets[:], offs)
+        nc.sync.dma_start(q_raw[:], qT[0].rearrange("(p j) w -> p j w", j=PACK))
         for r in range(4):
             nc.sync.dma_start(scale_win[r:P:32, :].bitcast(I32), k_scales[0, r:16:4, :].bitcast(I32))
-        nc.sync.dma_start(q_raw[:], qT[0].rearrange("(p j) w -> p j w", j=PACK))
         nc.sync.dma_start(nb_win[0:1, :], nb[0:1, :])
         nc.sync.dma_start(word_win[:].bitcast(I32), k_words[0].rearrange("p n t -> p (n t)").bitcast(I32))
 

@@ -21,6 +21,7 @@ U16 = mybir.dt.uint16
 U8 = mybir.dt.uint8
 FP8X4 = mybir.dt.float8_e4m3fn_x4
 ALU = mybir.AluOpType
+ACT = mybir.ActivationFunctionType
 
 
 def tile_attend_neu_scat_topk_kernel(tc, qT, k_words, k_scales, nb, offs, out):
@@ -37,30 +38,28 @@ def tile_attend_neu_scat_topk_kernel(tc, qT, k_words, k_scales, nb, offs, out):
         nb_win = shared.tile([P, T], F32, name="nb_win", offset=0, align_bytes=64)
         out_win = sb.tile([P, T], F32, name="out_win")
         ident = sb.tile([P, P], F32, name="ident")
+        live = P - 1
 
         def half_list(h):
             return offsets[:, h * (HALF // 16) : (h + 1) * (HALF // 16)]
 
         nc.vector.memset(scale_win[:].bitcast(I32), 0)
-        nc.vector.memset(nb_win[:].bitcast(I32), 0)
+        nc.vector.memset(nb_win[0:live, :].bitcast(I32), 0)
         nc.vector.memset(ident[:], 0.0)
         nc.vector.memset(out_win[:].bitcast(I32), 0)
         make_identity(nc, ident[:], nomemset=True)
 
         nc.sync.dma_start(offsets[:], offs)
+        nc.sync.dma_start(nb_win[live:P, :], nb[0:1, :])
         nc.sync.dma_start(q_raw[:], qT[0].rearrange("(p j) w -> p j w", j=PACK))
         for r in range(4):
             nc.sync.dma_start(scale_win[r:P:32, :].bitcast(I32), k_scales[0, r:16:4, :].bitcast(I32))
-        nc.sync.dma_start(nb_win[0:1, :], nb[0:1, :])
         nc.sync.dma_start(word_win[:].bitcast(I32), k_words[0].rearrange("p n t -> p (n t)").bitcast(I32))
 
         q_bf = sb.tile([P, NQ, PACK], BF16, name="q_bf", align_bytes=64)
         nc.scalar.copy(q_bf[:], q_raw[:].rearrange("p j w -> p w j"))
 
-        k_sc0 = sb.tile([P, HALF], U8, name="k_sc0", align_bytes=64)
-        nc.vector.tensor_copy(k_sc0[:], scale_win[:].indirect(half_list(0)))
-
-        bias = []
+        bias = sb.tile([P, N], F32, name="bias")
         for h in range(2):
             nb_row = sb.tile([P, HALF], F32, name=f"nb_row{h}")
             nc.vector.tensor_copy(nb_row[:], nb_win[:].indirect(half_list(h)))
@@ -68,17 +67,14 @@ def tile_attend_neu_scat_topk_kernel(tc, qT, k_words, k_scales, nb, offs, out):
             for c in range(2):
                 nc.tensor.transpose(turned[:, c, :], nb_row[:, c * P : (c + 1) * P], ident[:])
             nb_col = sb.tile([P, 2], F32, name=f"nb_col{h}")
-            nc.scalar.copy(nb_col[:], turned[:, :, 0])
+            nc.scalar.copy(nb_col[:], turned[:, :, live])
             spread = ps.tile([P, 2, P], F32, name=f"spread{h}")
             for c in range(2):
                 nc.tensor.transpose(spread[:, c, :], nb_col[:, c : c + 1].to_broadcast([P, P]), ident[:])
-            b = sb.tile([P, HALF], F32, name=f"bias{h}")
-            nc.scalar.copy(b[:], spread[:].rearrange("p c s -> p (c s)"))
-            bias.append(b)
+            nc.scalar.copy(bias[:, h * HALF : (h + 1) * HALF], spread[:].rearrange("p c s -> p (c s)"))
 
-        k_sc1 = shared.tile([P, HALF], U8, name="k_sc1", offset=0, align_bytes=64)
-        nc.vector.tensor_copy(k_sc1[:], scale_win[:].indirect(half_list(1)))
-        k_sc = [k_sc0, k_sc1]
+        k_sc = sb.tile([P, N], U8, name="k_sc", align_bytes=64)
+        nc.vector.tensor_copy(k_sc[:], scale_win[:].indirect(offsets[:]))
         q_codes = shared.tile([P, NQ], U32, name="q_codes", offset=512, align_bytes=64)
         q_sc = sb.tile([P, NQ], U8, name="q_sc", align_bytes=64)
         nc.vector.quantize_mx(out=q_codes[:].bitcast(FP8X4), scales=q_sc[:], in_=q_bf[:].rearrange("p w j -> p (w j)"))
@@ -93,20 +89,16 @@ def tile_attend_neu_scat_topk_kernel(tc, qT, k_words, k_scales, nb, offs, out):
                 lhsT=q_codes[:].bitcast(FP8X4),
                 lhsT_scale=q_sc[:],
                 rhs=k_codes[:].bitcast(FP8X4),
-                rhs_scale=k_sc[h][:],
+                rhs_scale=k_sc[:, h * HALF : (h + 1) * HALF],
                 start=True,
                 stop=True,
             )
             acc.append(a)
 
-        pre = []
+        floor = sb.tile([P, N], F32, name="floor")
         for h in range(2):
-            s = sb.tile([P, HALF], F32, name=f"pre{h}")
-            nc.vector.tensor_tensor(s[:], acc[h][:], bias[h][:], ALU.add)
-            pre.append(s)
-        y = sb.tile([P, N], F32, name="y")
-        for h in range(2):
-            nc.vector.tensor_scalar_max(y[:, h * HALF : (h + 1) * HALF], pre[h][:], 0.0)
-        nc.vector.tensor_copy(out_win[:].indirect(offsets[:]), y[:])
+            cols = slice(h * HALF, (h + 1) * HALF)
+            nc.vector.scalar_tensor_tensor(floor[:, cols], bias[:, cols], -1.0, acc[h][:], ALU.mult, ALU.max)
+        nc.vector.tensor_tensor(out_win[:].indirect(offsets[:]), floor[:], bias[:], ALU.add)
 
         nc.sync.dma_start(out[0], out_win[:])

@@ -79,26 +79,43 @@ def tile_attend_neu_scat_topk_kernel(tc, qT, k_words, k_scales, nb, offs, out):
         q_sc = sb.tile([P, NQ], U8, name="q_sc", align_bytes=64)
         nc.vector.quantize_mx(out=q_codes[:].bitcast(FP8X4), scales=q_sc[:], in_=q_bf[:].rearrange("p w j -> p (w j)"))
 
-        acc = []
+        k_codes = []
         for h in range(2):
-            k_codes = shared.tile([P, HALF], U32, name=f"k_codes{h}", offset=1024 * (h + 1), align_bytes=64)
-            nc.vector.tensor_copy(k_codes[:], word_win[:].indirect(half_list(h)))
-            a = ps.tile([P, HALF], F32, name=f"acc{h}", tag=("turned1", "spread0")[h])
+            kc = shared.tile([P, HALF], U32, name=f"k_codes{h}", offset=1024 * (h + 1), align_bytes=64)
+            nc.vector.tensor_copy(kc[:], word_win[:].indirect(half_list(h)))
+            k_codes.append(kc)
+
+        floor = sb.tile([P, N], F32, name="floor")
+
+        def multiply(lo, hi, tag):
+            h = lo // HALF
+            a = ps.tile([P, hi - lo], F32, name=f"acc{lo}", tag=tag)
             nc.tensor.matmul_mx(
                 out=a[:],
                 lhsT=q_codes[:].bitcast(FP8X4),
                 lhsT_scale=q_sc[:],
-                rhs=k_codes[:].bitcast(FP8X4),
-                rhs_scale=k_sc[:, h * HALF : (h + 1) * HALF],
+                rhs=k_codes[h][:, lo - h * HALF : hi - h * HALF].bitcast(FP8X4),
+                rhs_scale=k_sc[:, lo:hi],
                 start=True,
                 stop=True,
             )
-            acc.append(a)
+            return a
 
-        floor = sb.tile([P, N], F32, name="floor")
-        for h in range(2):
-            cols = slice(h * HALF, (h + 1) * HALF)
-            nc.vector.scalar_tensor_tensor(floor[:, cols], bias[:, cols], -1.0, acc[h][:], ALU.mult, ALU.max)
-        nc.vector.tensor_tensor(out_win[:].indirect(offsets[:]), floor[:], bias[:], ALU.add)
+        def clamp(a, lo, hi):
+            nc.vector.scalar_tensor_tensor(floor[:, lo:hi], bias[:, lo:hi], -1.0, a[:], ALU.mult, ALU.max)
+
+        def scatter(lo, hi):
+            nc.vector.tensor_tensor(
+                out_win[:].indirect(offsets[:, lo // 16 : hi // 16]), floor[:, lo:hi], bias[:, lo:hi], ALU.add
+            )
+
+        first = multiply(0, P, "turned1")
+        second = multiply(P, HALF, "spread0")
+        clamp(first, 0, P)
+        clamp(second, P, HALF)
+        scatter(0, P)
+        third = multiply(HALF, N, "turned1")
+        clamp(third, HALF, N)
+        scatter(P, N)
 
         nc.sync.dma_start(out[0], out_win[:])

@@ -53,7 +53,7 @@ def tile_attend_neu_scat_topk_kernel(tc, qT, k_words, k_scales, nb, offs, out):
         nc.sync.dma_start(nb_win[live:P, :], nb[0:1, :])
         nc.sync.dma_start(q_raw[:], qT[0].rearrange("(p j) w -> p j w", j=PACK))
         for r in range(4):
-            nc.sync.dma_start(scale_win[r:P:32, :].bitcast(I32), k_scales[0, r:16:4, :].bitcast(I32))
+            (nc.scalar if r == 0 else nc.sync).dma_start(scale_win[r:P:32, :].bitcast(I32), k_scales[0, r:16:4, :].bitcast(I32))
         nc.sync.dma_start(word_win[:].bitcast(I32), k_words[0].rearrange("p n t -> p (n t)").bitcast(I32))
 
         q_bf = sb.tile([P, NQ, PACK], BF16, name="q_bf", align_bytes=64)

@@ -50,7 +50,7 @@ def tile_attend_neu_scat_topk_kernel(tc, qT, k_words, k_scales, nb, offs, out):
         make_identity(nc, ident[:], nomemset=True)
 
         nc.sync.dma_start(offsets[:], offs)
-        nc.sync.dma_start(nb_win[live:P, :], nb[0:1, :])
+        nc.scalar.dma_start(nb_win[live:P, :], nb[0:1, :])
         nc.sync.dma_start(q_raw[:], qT[0].rearrange("(p j) w -> p j w", j=PACK))
         for r in range(4):
             (nc.scalar if r == 0 else nc.sync).dma_start(scale_win[r:P:32, :].bitcast(I32), k_scales[0, r:16:4, :].bitcast(I32))

@@ -59,19 +59,27 @@ def tile_attend_neu_scat_topk_kernel(tc, qT, k_words, k_scales, nb, offs, out):
         q_bf = sb.tile([P, NQ, PACK], BF16, name="q_bf", align_bytes=64)
         nc.scalar.copy(q_bf[:], q_raw[:].rearrange("p j w -> p w j"))
 
-        bias = sb.tile([P, N], F32, name="bias")
+        bias = sb.tile([P, HALF], F32, name="bias")
+        nb_rows = []
         for h in range(2):
             nb_row = sb.tile([P, HALF], F32, name=f"nb_row{h}")
             nc.vector.tensor_copy(nb_row[:], nb_win[:].indirect(half_list(h)))
-            turned = ps.tile([P, 2, P], F32, name=f"turned{h}")
+            nb_rows.append(nb_row)
+
+        def to_columns(h):
+            turned = ps.tile([P, 2, P], F32, name=f"turned{h}", tag="turned")
             for c in range(2):
-                nc.tensor.transpose(turned[:, c, :], nb_row[:, c * P : (c + 1) * P], ident[:])
+                nc.tensor.transpose(turned[:, c, :], nb_rows[h][:, c * P : (c + 1) * P], ident[:])
             nb_col = sb.tile([P, 2], F32, name=f"nb_col{h}")
             nc.scalar.copy(nb_col[:], turned[:, :, live])
-            spread = ps.tile([P, 2, P], F32, name=f"spread{h}")
-            for c in range(2):
-                nc.tensor.transpose(spread[:, c, :], nb_col[:, c : c + 1].to_broadcast([P, P]), ident[:])
-            nc.scalar.copy(bias[:, h * HALF : (h + 1) * HALF], spread[:].rearrange("p c s -> p (c s)"))
+            return nb_col
+
+        col0 = to_columns(0)
+        for c in range(2):
+            spread = ps.tile([P, P], F32, name=f"spread{c}")
+            nc.tensor.transpose(spread[:], col0[:, c : c + 1].to_broadcast([P, P]), ident[:])
+            nc.scalar.copy(bias[:, c * P : (c + 1) * P], spread[:])
+        col1 = to_columns(1)
 
         k_sc = sb.tile([P, N], U8, name="k_sc", align_bytes=64)
         nc.vector.tensor_copy(k_sc[:], scale_win[:].indirect(offsets[:]))
@@ -85,37 +93,41 @@ def tile_attend_neu_scat_topk_kernel(tc, qT, k_words, k_scales, nb, offs, out):
             nc.vector.tensor_copy(kc[:], word_win[:].indirect(half_list(h)))
             k_codes.append(kc)
 
-        floor = sb.tile([P, N], F32, name="floor")
-
-        def multiply(lo, hi, tag):
-            h = lo // HALF
-            a = ps.tile([P, hi - lo], F32, name=f"acc{lo}", tag=tag)
+        floor = sb.tile([P, HALF], F32, name="floor")
+        for c in range(2):
+            cols = slice(c * P, (c + 1) * P)
+            a = ps.tile([P, P], F32, name=f"acc{c}", tag=f"spread{c}")
             nc.tensor.matmul_mx(
                 out=a[:],
                 lhsT=q_codes[:].bitcast(FP8X4),
                 lhsT_scale=q_sc[:],
-                rhs=k_codes[h][:, lo - h * HALF : hi - h * HALF].bitcast(FP8X4),
-                rhs_scale=k_sc[:, lo:hi],
+                rhs=k_codes[0][:, cols].bitcast(FP8X4),
+                rhs_scale=k_sc[:, cols],
                 start=True,
                 stop=True,
             )
-            return a
+            nc.vector.scalar_tensor_tensor(floor[:, cols], bias[:, cols], -1.0, a[:], ALU.mult, ALU.max)
 
-        def clamp(a, lo, hi):
-            nc.vector.scalar_tensor_tensor(floor[:, lo:hi], bias[:, lo:hi], -1.0, a[:], ALU.mult, ALU.max)
-
-        def scatter(lo, hi):
-            nc.vector.tensor_tensor(
-                out_win[:].indirect(offsets[:, lo // 16 : hi // 16]), floor[:, lo:hi], bias[:, lo:hi], ALU.add
+        by_slot = ps.tile([P, 2, P], F32, name="by_slot", tag="turned")
+        for c in range(2):
+            nc.tensor.matmul_mx(
+                out=by_slot[:, c, :],
+                lhsT=k_codes[1][:, c * P : (c + 1) * P].bitcast(FP8X4),
+                lhsT_scale=k_sc[:, HALF + c * P : HALF + (c + 1) * P],
+                rhs=q_codes[:].bitcast(FP8X4),
+                rhs_scale=q_sc[:],
+                start=True,
+                stop=True,
             )
+        y_slot = sb.tile([P, 2, P], F32, name="y_slot")
+        by_query = ps.tile([P, 2, P], F32, name="by_query")
+        for c in range(2):
+            nc.scalar.activation(y_slot[:, c, :], by_slot[:, c, :], ACT.Relu, bias=col1[:, c : c + 1])
+            nc.tensor.transpose(by_query[:, c, :], y_slot[:, c, :], ident[:])
+        y = sb.tile([P, HALF], F32, name="y")
+        nc.scalar.copy(y[:], by_query[:].rearrange("p c s -> p (c s)"))
 
-        first = multiply(0, P, "turned1")
-        second = multiply(P, HALF, "spread0")
-        clamp(first, 0, P)
-        clamp(second, P, HALF)
-        scatter(0, P)
-        third = multiply(HALF, N, "turned1")
-        clamp(third, HALF, N)
-        scatter(P, N)
+        nc.vector.tensor_tensor(out_win[:].indirect(half_list(0)), floor[:], bias[:], ALU.add)
+        nc.vector.tensor_copy(out_win[:].indirect(half_list(1)), y[:])
 
         nc.sync.dma_start(out[0], out_win[:])

@@ -1,7 +1,6 @@
 from contextlib import ExitStack
 
 import concourse.mybir as mybir
-from concourse.masks import make_identity
 
 P = 128
 T = 2048
@@ -10,6 +9,8 @@ D = 512
 NQ = 128
 PACK = 4
 HALF = N // 2
+ROW0 = 48
+EARLY = 512
 
 FLOPS = 2 * D * NQ * N
 
@@ -29,6 +30,7 @@ def tile_attend_neu_scat_topk_kernel(tc, qT, k_words, k_scales, nb, offs, out):
     with ExitStack() as ctx:
         sb = ctx.enter_context(tc.tile_pool(name="sb", bufs=1))
         shared = ctx.enter_context(tc.tile_pool(name="shared", bufs=1))
+        early = ctx.enter_context(tc.tile_pool(name="early", bufs=1))
         ps = ctx.enter_context(tc.psum_pool(name="ps", bufs=1))
 
         offsets = sb.tile([P, N // 16], U16, name="offsets")
@@ -43,33 +45,51 @@ def tile_attend_neu_scat_topk_kernel(tc, qT, k_words, k_scales, nb, offs, out):
         def half_list(h):
             return offsets[:, h * (HALF // 16) : (h + 1) * (HALF // 16)]
 
-        nc.vector.memset(scale_win[:].bitcast(I32), 0)
+        k_sc = sb.tile([P, N], U8, name="k_sc", align_bytes=64)
+        zeros = early.tile([P, P], F32, name="zeros", offset=1792, align_bytes=64)
+        nc.vector.memset(zeros[:], 0.0)
+        nc.gpsimd.affine_select(
+            out=ident[:],
+            in_=zeros[:],
+            compare_op=ALU.not_equal,
+            fill=1.0,
+            base=0,
+            pattern=[[-1, P]],
+            channel_multiplier=1,
+        )
+        nc.vector.memset(scale_win[0:ROW0, :].bitcast(I32), 0)
+        nc.vector.memset(scale_win[ROW0 + 16 : P, :].bitcast(I32), 0)
+        nc.vector.memset(k_sc[:].bitcast(I32), 0)
         nc.vector.memset(nb_win[0:live, :].bitcast(I32), 0)
-        nc.vector.memset(ident[:], 0.0)
-        nc.vector.memset(out_win[:].bitcast(I32), 0)
-        make_identity(nc, ident[:], nomemset=True)
+        nc.vector.memset(out_win[:, 0:EARLY].bitcast(I32), 0)
+        nc.gpsimd.memset(out_win[:, EARLY - 16 : T].bitcast(I32), 0)
 
         nc.sync.dma_start(offsets[:], offs)
         nc.scalar.dma_start(nb_win[live:P, :], nb[0:1, :])
+        nc.sync.dma_start(scale_win[ROW0 : ROW0 + 16, :].bitcast(I32), k_scales[0].bitcast(I32))
         nc.sync.dma_start(q_raw[:], qT[0].rearrange("(p j) w -> p j w", j=PACK))
-        for r in range(4):
-            (nc.scalar if r == 0 else nc.sync).dma_start(scale_win[r:P:32, :].bitcast(I32), k_scales[0, r:16:4, :].bitcast(I32))
         nc.sync.dma_start(word_win[:].bitcast(I32), k_words[0].rearrange("p n t -> p (n t)").bitcast(I32))
 
         q_bf = sb.tile([P, NQ, PACK], BF16, name="q_bf", align_bytes=64)
         nc.scalar.copy(q_bf[:], q_raw[:].rearrange("p j w -> p w j"))
 
         bias = sb.tile([P, HALF], F32, name="bias")
-        nb_rows = []
+        nb_rows = early.tile([P, N], F32, name="nb_rows", offset=0, align_bytes=64)
+        picked = early.tile([P, N], U8, name="picked", offset=2048, align_bytes=64)
         for h in range(2):
-            nb_row = sb.tile([P, HALF], F32, name=f"nb_row{h}")
-            nc.vector.tensor_copy(nb_row[:], nb_win[:].indirect(half_list(h)))
-            nb_rows.append(nb_row)
+            slots = slice(h * HALF, (h + 1) * HALF)
+            nc.vector.tensor_copy(picked[:, slots], scale_win[:].indirect(half_list(h)))
+            for a in range(4):
+                nc.sync.dma_start(
+                    k_sc[32 * a : 32 * a + 4, slots].bitcast(I32),
+                    picked[ROW0 + 4 * a : ROW0 + 4 * a + 4, slots].bitcast(I32),
+                )
+            nc.vector.tensor_copy(nb_rows[:, slots], nb_win[:].indirect(half_list(h)))
 
         def to_columns(h):
             turned = ps.tile([P, 2, P], F32, name=f"turned{h}", tag="turned")
             for c in range(2):
-                nc.tensor.transpose(turned[:, c, :], nb_rows[h][:, c * P : (c + 1) * P], ident[:])
+                nc.tensor.transpose(turned[:, c, :], nb_rows[:, h * HALF + c * P : h * HALF + (c + 1) * P], ident[:])
             nb_col = sb.tile([P, 2], F32, name=f"nb_col{h}")
             nc.scalar.copy(nb_col[:], turned[:, :, live])
             return nb_col
@@ -81,8 +101,6 @@ def tile_attend_neu_scat_topk_kernel(tc, qT, k_words, k_scales, nb, offs, out):
             nc.scalar.copy(bias[:, c * P : (c + 1) * P], spread[:])
         col1 = to_columns(1)
 
-        k_sc = sb.tile([P, N], U8, name="k_sc", align_bytes=64)
-        nc.vector.tensor_copy(k_sc[:], scale_win[:].indirect(offsets[:]))
         q_codes = shared.tile([P, NQ], U32, name="q_codes", offset=512, align_bytes=64)
         q_sc = sb.tile([P, NQ], U8, name="q_sc", align_bytes=64)
         nc.vector.quantize_mx(out=q_codes[:].bitcast(FP8X4), scales=q_sc[:], in_=q_bf[:].rearrange("p w j -> p (w j)"))
@@ -96,7 +114,7 @@ def tile_attend_neu_scat_topk_kernel(tc, qT, k_words, k_scales, nb, offs, out):
         floor = sb.tile([P, HALF], F32, name="floor")
         for c in range(2):
             cols = slice(c * P, (c + 1) * P)
-            a = ps.tile([P, P], F32, name=f"acc{c}", tag=f"spread{c}")
+            a = ps.tile([P, P], F32, name=f"acc{c}")
             nc.tensor.matmul_mx(
                 out=a[:],
                 lhsT=q_codes[:].bitcast(FP8X4),

@@ -10,7 +10,7 @@ NQ = 128
 PACK = 4
 HALF = N // 2
 ROW0 = 48
-EARLY = 512
+EARLY = 256
 
 FLOPS = 2 * D * NQ * N
 
@@ -76,14 +76,22 @@ def tile_attend_neu_scat_topk_kernel(tc, qT, k_words, k_scales, nb, offs, out):
         bias = sb.tile([P, HALF], F32, name="bias")
         nb_rows = early.tile([P, N], F32, name="nb_rows", offset=0, align_bytes=64)
         picked = early.tile([P, N], U8, name="picked", offset=2048, align_bytes=64)
+
+        def to_plane(a, slots):
+            nc.sync.dma_start(
+                k_sc[32 * a : 32 * a + 4, slots].bitcast(I32),
+                picked[ROW0 + 4 * a : ROW0 + 4 * a + 4, slots].bitcast(I32),
+            )
+
         for h in range(2):
             slots = slice(h * HALF, (h + 1) * HALF)
             nc.vector.tensor_copy(picked[:, slots], scale_win[:].indirect(half_list(h)))
-            for a in range(4):
-                nc.sync.dma_start(
-                    k_sc[32 * a : 32 * a + 4, slots].bitcast(I32),
-                    picked[ROW0 + 4 * a : ROW0 + 4 * a + 4, slots].bitcast(I32),
-                )
+            if h == 1:
+                to_plane(3, slice(0, N))
+            for a in range(3):
+                to_plane(a, slots)
+        for h in range(2):
+            slots = slice(h * HALF, (h + 1) * HALF)
             nc.vector.tensor_copy(nb_rows[:, slots], nb_win[:].indirect(half_list(h)))
 
         def to_columns(h):

@@ -10,7 +10,7 @@ NQ = 128
 PACK = 4
 HALF = N // 2
 ROW0 = 48
-EARLY = 256
+BANK = 2048
 
 FLOPS = 2 * D * NQ * N
 
@@ -37,16 +37,19 @@ def tile_attend_neu_scat_topk_kernel(tc, qT, k_words, k_scales, nb, offs, out):
         q_raw = sb.tile([P, PACK, NQ], F32, name="q_raw")
         scale_win = sb.tile([P, T], U8, name="scale_win", align_bytes=64)
         word_win = sb.tile([P, T], U32, name="word_win", align_bytes=64)
-        nb_win = shared.tile([P, T], F32, name="nb_win", offset=0, align_bytes=64)
-        out_win = sb.tile([P, T], F32, name="out_win")
+        nb_win = sb.tile([P, T], F32, name="nb_win")
         ident = sb.tile([P, P], F32, name="ident")
+        k_sc = sb.tile([P, N], U8, name="k_sc", align_bytes=64)
+        zeros = early.tile([P, P], F32, name="zeros", offset=960, align_bytes=64)
         live = P - 1
 
         def half_list(h):
             return offsets[:, h * (HALF // 16) : (h + 1) * (HALF // 16)]
 
-        k_sc = sb.tile([P, N], U8, name="k_sc", align_bytes=64)
-        zeros = early.tile([P, P], F32, name="zeros", offset=1792, align_bytes=64)
+        nc.vector.memset(scale_win[0:ROW0, :].bitcast(I32), 0)
+        nc.vector.memset(scale_win[ROW0 + 16 : P, :].bitcast(I32), 0)
+        nc.vector.memset(k_sc[:].bitcast(I32), 0)
+        nc.vector.memset(nb_win[0:live, :].bitcast(I32), 0)
         nc.vector.memset(zeros[:], 0.0)
         nc.gpsimd.affine_select(
             out=ident[:],
@@ -57,12 +60,6 @@ def tile_attend_neu_scat_topk_kernel(tc, qT, k_words, k_scales, nb, offs, out):
             pattern=[[-1, P]],
             channel_multiplier=1,
         )
-        nc.vector.memset(scale_win[0:ROW0, :].bitcast(I32), 0)
-        nc.vector.memset(scale_win[ROW0 + 16 : P, :].bitcast(I32), 0)
-        nc.vector.memset(k_sc[:].bitcast(I32), 0)
-        nc.vector.memset(nb_win[0:live, :].bitcast(I32), 0)
-        nc.vector.memset(out_win[:, 0:EARLY].bitcast(I32), 0)
-        nc.gpsimd.memset(out_win[:, EARLY - 16 : T].bitcast(I32), 0)
 
         nc.sync.dma_start(offsets[:], offs)
         nc.scalar.dma_start(nb_win[live:P, :], nb[0:1, :])
@@ -70,59 +67,61 @@ def tile_attend_neu_scat_topk_kernel(tc, qT, k_words, k_scales, nb, offs, out):
         nc.sync.dma_start(q_raw[:], qT[0].rearrange("(p j) w -> p j w", j=PACK))
         nc.sync.dma_start(word_win[:].bitcast(I32), k_words[0].rearrange("p n t -> p (n t)").bitcast(I32))
 
-        q_bf = sb.tile([P, NQ, PACK], BF16, name="q_bf", align_bytes=64)
+        q_bf = shared.tile([P, NQ, PACK], BF16, name="q_bf", offset=0, align_bytes=64)
         nc.scalar.copy(q_bf[:], q_raw[:].rearrange("p j w -> p w j"))
 
-        bias = sb.tile([P, HALF], F32, name="bias")
-        nb_rows = early.tile([P, N], F32, name="nb_rows", offset=0, align_bytes=64)
-        picked = early.tile([P, N], U8, name="picked", offset=2048, align_bytes=64)
+        def pick_scales(h, picked):
+            nc.vector.tensor_copy(picked[:], scale_win[:].indirect(half_list(h)))
+            for a in range(4):
+                nc.sync.dma_start(
+                    k_sc[32 * a : 32 * a + 4, h * HALF : (h + 1) * HALF].bitcast(I32),
+                    picked[ROW0 + 4 * a : ROW0 + 4 * a + 4, :].bitcast(I32),
+                )
 
-        def to_plane(a, slots):
-            nc.sync.dma_start(
-                k_sc[32 * a : 32 * a + 4, slots].bitcast(I32),
-                picked[ROW0 + 4 * a : ROW0 + 4 * a + 4, slots].bitcast(I32),
-            )
+        picked0 = sb.tile([P, HALF], U8, name="picked0", align_bytes=64)
+        pick_scales(0, picked0)
+        nb_row0 = sb.tile([P, HALF], F32, name="nb_row0")
+        nc.vector.tensor_copy(nb_row0[:], nb_win[:].indirect(half_list(0)))
+        picked1 = early.tile([P, HALF], U8, name="picked1", offset=1152, align_bytes=64)
+        pick_scales(1, picked1)
 
-        for h in range(2):
-            slots = slice(h * HALF, (h + 1) * HALF)
-            nc.vector.tensor_copy(picked[:, slots], scale_win[:].indirect(half_list(h)))
-            if h == 1:
-                to_plane(3, slice(0, N))
-            for a in range(3):
-                to_plane(a, slots)
-        for h in range(2):
-            slots = slice(h * HALF, (h + 1) * HALF)
-            nc.vector.tensor_copy(nb_rows[:, slots], nb_win[:].indirect(half_list(h)))
-
-        def to_columns(h):
-            turned = ps.tile([P, 2, P], F32, name=f"turned{h}", tag="turned")
-            for c in range(2):
-                nc.tensor.transpose(turned[:, c, :], nb_rows[:, h * HALF + c * P : h * HALF + (c + 1) * P], ident[:])
-            nb_col = sb.tile([P, 2], F32, name=f"nb_col{h}")
-            nc.scalar.copy(nb_col[:], turned[:, :, live])
-            return nb_col
-
-        col0 = to_columns(0)
-        for c in range(2):
-            spread = ps.tile([P, P], F32, name=f"spread{c}")
-            nc.tensor.transpose(spread[:], col0[:, c : c + 1].to_broadcast([P, P]), ident[:])
-            nc.scalar.copy(bias[:, c * P : (c + 1) * P], spread[:])
-        col1 = to_columns(1)
-
-        q_codes = shared.tile([P, NQ], U32, name="q_codes", offset=512, align_bytes=64)
-        q_sc = sb.tile([P, NQ], U8, name="q_sc", align_bytes=64)
+        q_codes = sb.tile([P, NQ], U32, name="q_codes", align_bytes=64)
+        q_sc = early.tile([P, NQ], U8, name="q_sc", offset=1024, align_bytes=64)
         nc.vector.quantize_mx(out=q_codes[:].bitcast(FP8X4), scales=q_sc[:], in_=q_bf[:].rearrange("p w j -> p (w j)"))
+        out_win = shared.tile([P, T], F32, name="out_win", offset=0, align_bytes=64)
+        nc.gpsimd.memset(out_win[:].bitcast(I32), 0)
 
-        k_codes = []
+        nb_row1 = early.tile([P, HALF], F32, name="nb_row1", offset=0, align_bytes=64)
+        nc.vector.tensor_copy(nb_row1[:], nb_win[:].indirect(half_list(1)))
+        nb_rows = [nb_row0, nb_row1]
+
+        bias = sb.tile([P, HALF], F32, name="bias")
+        cols0 = []
+        for c in range(2):
+            turned = ps.tile([P, (P, 4 * 512)[c]], F32, name=f"turned0_{c}", offset=(7 * BANK, 0)[c])
+            nc.tensor.transpose(turned[:, 0:P], nb_rows[0][:, c * P : (c + 1) * P], ident[:])
+            nb_col = sb.tile([P, 1], F32, name=f"nb_col0_{c}")
+            nc.scalar.copy(nb_col[:], turned[:, live:P])
+            cols0.append(nb_col)
+        for c in range(2):
+            spread = ps.tile([P, P], F32, name=f"spread{c}", offset=(4 + c) * BANK)
+            nc.tensor.transpose(spread[:], cols0[c][:].to_broadcast([P, P]), ident[:])
+            nc.scalar.copy(bias[:, c * P : (c + 1) * P], spread[:])
+        turned1 = ps.tile([P, 2, P], F32, name="turned1", offset=2 * BANK)
+        for c in range(2):
+            nc.tensor.transpose(turned1[:, c, :], nb_rows[1][:, c * P : (c + 1) * P], ident[:])
+        col1 = sb.tile([P, 2], F32, name="col1")
+        nc.scalar.copy(col1[:], turned1[:, :, live])
+
+        k_all = early.tile([P, N], U32, name="k_all", offset=1408, align_bytes=64)
+        k_codes = [k_all[:, 0:HALF], k_all[:, HALF:N]]
         for h in range(2):
-            kc = shared.tile([P, HALF], U32, name=f"k_codes{h}", offset=1024 * (h + 1), align_bytes=64)
-            nc.vector.tensor_copy(kc[:], word_win[:].indirect(half_list(h)))
-            k_codes.append(kc)
+            nc.vector.tensor_copy(k_codes[h], word_win[:].indirect(half_list(h)))
 
         floor = sb.tile([P, HALF], F32, name="floor")
         for c in range(2):
             cols = slice(c * P, (c + 1) * P)
-            a = ps.tile([P, P], F32, name=f"acc{c}")
+            a = ps.tile([P, P], F32, name=f"acc{c}", offset=c * BANK)
             nc.tensor.matmul_mx(
                 out=a[:],
                 lhsT=q_codes[:].bitcast(FP8X4),
@@ -134,7 +133,7 @@ def tile_attend_neu_scat_topk_kernel(tc, qT, k_words, k_scales, nb, offs, out):
             )
             nc.vector.scalar_tensor_tensor(floor[:, cols], bias[:, cols], -1.0, a[:], ALU.mult, ALU.max)
 
-        by_slot = ps.tile([P, 2, P], F32, name="by_slot", tag="turned")
+        by_slot = ps.tile([P, 2, P], F32, name="by_slot", offset=3 * BANK)
         for c in range(2):
             nc.tensor.matmul_mx(
                 out=by_slot[:, c, :],
@@ -146,7 +145,7 @@ def tile_attend_neu_scat_topk_kernel(tc, qT, k_words, k_scales, nb, offs, out):
                 stop=True,
             )
         y_slot = sb.tile([P, 2, P], F32, name="y_slot")
-        by_query = ps.tile([P, 2, P], F32, name="by_query")
+        by_query = ps.tile([P, 2, P], F32, name="by_query", offset=6 * BANK)
         for c in range(2):
             nc.scalar.activation(y_slot[:, c, :], by_slot[:, c, :], ACT.Relu, bias=col1[:, c : c + 1])
             nc.tensor.transpose(by_query[:, c, :], y_slot[:, c, :], ident[:])

@@ -10,6 +10,7 @@ NQ = 128
 PACK = 4
 HALF = N // 2
 ROW0 = 48
+LATE = 448
 BANK = 2048
 
 FLOPS = 2 * D * NQ * N
@@ -29,7 +30,6 @@ def tile_attend_neu_scat_topk_kernel(tc, qT, k_words, k_scales, nb, offs, out):
     nc = tc.nc
     with ExitStack() as ctx:
         sb = ctx.enter_context(tc.tile_pool(name="sb", bufs=1))
-        shared = ctx.enter_context(tc.tile_pool(name="shared", bufs=1))
         early = ctx.enter_context(tc.tile_pool(name="early", bufs=1))
         ps = ctx.enter_context(tc.psum_pool(name="ps", bufs=1))
 
@@ -40,7 +40,7 @@ def tile_attend_neu_scat_topk_kernel(tc, qT, k_words, k_scales, nb, offs, out):
         nb_win = sb.tile([P, T], F32, name="nb_win")
         ident = sb.tile([P, P], F32, name="ident")
         k_sc = sb.tile([P, N], U8, name="k_sc", align_bytes=64)
-        zeros = early.tile([P, P], F32, name="zeros", offset=960, align_bytes=64)
+        zeros = early.tile([P, 3 * P], F32, name="zeros", offset=1984, align_bytes=64)
         live = P - 1
 
         def half_list(h):
@@ -50,16 +50,18 @@ def tile_attend_neu_scat_topk_kernel(tc, qT, k_words, k_scales, nb, offs, out):
         nc.vector.memset(scale_win[ROW0 + 16 : P, :].bitcast(I32), 0)
         nc.vector.memset(k_sc[:].bitcast(I32), 0)
         nc.vector.memset(nb_win[0:live, :].bitcast(I32), 0)
-        nc.vector.memset(zeros[:], 0.0)
+        nc.vector.memset(zeros[:, 0:P], 0.0)
         nc.gpsimd.affine_select(
             out=ident[:],
-            in_=zeros[:],
+            in_=zeros[:, 0:P],
             compare_op=ALU.not_equal,
             fill=1.0,
             base=0,
             pattern=[[-1, P]],
             channel_multiplier=1,
         )
+        out_win = early.tile([P, T], F32, name="out_win", offset=3456, align_bytes=64)
+        nc.gpsimd.memset(out_win[:, 0 : T - LATE].bitcast(I32), 0)
 
         nc.sync.dma_start(offsets[:], offs)
         nc.scalar.dma_start(nb_win[live:P, :], nb[0:1, :])
@@ -67,7 +69,7 @@ def tile_attend_neu_scat_topk_kernel(tc, qT, k_words, k_scales, nb, offs, out):
         nc.sync.dma_start(q_raw[:], qT[0].rearrange("(p j) w -> p j w", j=PACK))
         nc.sync.dma_start(word_win[:].bitcast(I32), k_words[0].rearrange("p n t -> p (n t)").bitcast(I32))
 
-        q_bf = shared.tile([P, NQ, PACK], BF16, name="q_bf", offset=0, align_bytes=64)
+        q_bf = sb.tile([P, NQ, PACK], BF16, name="q_bf", align_bytes=64)
         nc.scalar.copy(q_bf[:], q_raw[:].rearrange("p j w -> p w j"))
 
         def pick_scales(h, picked):
@@ -82,18 +84,16 @@ def tile_attend_neu_scat_topk_kernel(tc, qT, k_words, k_scales, nb, offs, out):
         pick_scales(0, picked0)
         nb_row0 = sb.tile([P, HALF], F32, name="nb_row0")
         nc.vector.tensor_copy(nb_row0[:], nb_win[:].indirect(half_list(0)))
-        picked1 = early.tile([P, HALF], U8, name="picked1", offset=1152, align_bytes=64)
+        picked1 = early.tile([P, HALF], U8, name="picked1", offset=3200, align_bytes=64)
         pick_scales(1, picked1)
 
-        q_codes = sb.tile([P, NQ], U32, name="q_codes", align_bytes=64)
-        q_sc = early.tile([P, NQ], U8, name="q_sc", offset=1024, align_bytes=64)
-        nc.vector.quantize_mx(out=q_codes[:].bitcast(FP8X4), scales=q_sc[:], in_=q_bf[:].rearrange("p w j -> p (w j)"))
-        out_win = shared.tile([P, T], F32, name="out_win", offset=0, align_bytes=64)
-        nc.gpsimd.memset(out_win[:].bitcast(I32), 0)
-
-        nb_row1 = early.tile([P, HALF], F32, name="nb_row1", offset=0, align_bytes=64)
+        nb_row1 = early.tile([P, HALF], F32, name="nb_row1", offset=2048, align_bytes=64)
         nc.vector.tensor_copy(nb_row1[:], nb_win[:].indirect(half_list(1)))
         nb_rows = [nb_row0, nb_row1]
+
+        q_codes = sb.tile([P, NQ], U32, name="q_codes", align_bytes=64)
+        q_sc = early.tile([P, NQ], U8, name="q_sc", offset=3072, align_bytes=64)
+        nc.vector.quantize_mx(out=q_codes[:].bitcast(FP8X4), scales=q_sc[:], in_=q_bf[:].rearrange("p w j -> p (w j)"))
 
         bias = sb.tile([P, HALF], F32, name="bias")
         cols0 = []
@@ -113,10 +113,11 @@ def tile_attend_neu_scat_topk_kernel(tc, qT, k_words, k_scales, nb, offs, out):
         col1 = sb.tile([P, 2], F32, name="col1")
         nc.scalar.copy(col1[:], turned1[:, :, live])
 
-        k_all = early.tile([P, N], U32, name="k_all", offset=1408, align_bytes=64)
+        k_all = early.tile([P, N], U32, name="k_all", offset=0, align_bytes=64)
         k_codes = [k_all[:, 0:HALF], k_all[:, HALF:N]]
         for h in range(2):
             nc.vector.tensor_copy(k_codes[h], word_win[:].indirect(half_list(h)))
+        nc.vector.memset(out_win[:, T - LATE : T].bitcast(I32), 0)
 
         floor = sb.tile([P, HALF], F32, name="floor")
         for c in range(2):
@@ -133,10 +134,11 @@ def tile_attend_neu_scat_topk_kernel(tc, qT, k_words, k_scales, nb, offs, out):
             )
             nc.vector.scalar_tensor_tensor(floor[:, cols], bias[:, cols], -1.0, a[:], ALU.mult, ALU.max)
 
-        by_slot = ps.tile([P, 2, P], F32, name="by_slot", offset=3 * BANK)
+        by_slot = []
         for c in range(2):
+            b = ps.tile([P, P], F32, name=f"by_slot{c}", offset=(3, 5)[c] * BANK)
             nc.tensor.matmul_mx(
-                out=by_slot[:, c, :],
+                out=b[:],
                 lhsT=k_codes[1][:, c * P : (c + 1) * P].bitcast(FP8X4),
                 lhsT_scale=k_sc[:, HALF + c * P : HALF + (c + 1) * P],
                 rhs=q_codes[:].bitcast(FP8X4),
@@ -144,13 +146,15 @@ def tile_attend_neu_scat_topk_kernel(tc, qT, k_words, k_scales, nb, offs, out):
                 start=True,
                 stop=True,
             )
+            by_slot.append(b)
         y_slot = sb.tile([P, 2, P], F32, name="y_slot")
-        by_query = ps.tile([P, 2, P], F32, name="by_query", offset=6 * BANK)
-        for c in range(2):
-            nc.scalar.activation(y_slot[:, c, :], by_slot[:, c, :], ACT.Relu, bias=col1[:, c : c + 1])
-            nc.tensor.transpose(by_query[:, c, :], y_slot[:, c, :], ident[:])
         y = sb.tile([P, HALF], F32, name="y")
-        nc.scalar.copy(y[:], by_query[:].rearrange("p c s -> p (c s)"))
+        for c in range(2):
+            nc.scalar.activation(y_slot[:, c, :], by_slot[c][:], ACT.Relu, bias=col1[:, c : c + 1])
+        for c in range(2):
+            by_query = ps.tile([P, P], F32, name=f"by_query{c}", offset=(6 + c) * BANK)
+            nc.tensor.transpose(by_query[:], y_slot[:, c, :], ident[:])
+            nc.scalar.copy(y[:, c * P : (c + 1) * P], by_query[:])
 
         nc.vector.tensor_tensor(out_win[:].indirect(half_list(0)), floor[:], bias[:], ALU.add)
         nc.vector.tensor_copy(out_win[:].indirect(half_list(1)), y[:])

@@ -63,9 +63,9 @@ def tile_attend_neu_scat_topk_kernel(tc, qT, k_words, k_scales, nb, offs, out):
         out_win = early.tile([P, T], F32, name="out_win", offset=3456, align_bytes=64)
         nc.gpsimd.memset(out_win[:, 0 : T - LATE].bitcast(I32), 0)
 
-        nc.sync.dma_start(offsets[:], offs)
-        nc.scalar.dma_start(nb_win[live:P, :], nb[0:1, :])
         nc.sync.dma_start(scale_win[ROW0 : ROW0 + 16, :].bitcast(I32), k_scales[0].bitcast(I32))
+        nc.scalar.dma_start(nb_win[live:P, :], nb[0:1, :])
+        nc.sync.dma_start(offsets[:], offs)
         nc.sync.dma_start(q_raw[:], qT[0].rearrange("(p j) w -> p j w", j=PACK))
         nc.sync.dma_start(word_win[:].bitcast(I32), k_words[0].rearrange("p n t -> p (n t)").bitcast(I32))
 

@@ -10,8 +10,9 @@ NQ = 128
 PACK = 4
 HALF = N // 2
 ROW0 = 48
-LATE = 448
 BANK = 2048
+POOL_NB = 1048
+CHUNK = 256
 
 FLOPS = 2 * D * NQ * N
 
@@ -30,133 +31,106 @@ def tile_attend_neu_scat_topk_kernel(tc, qT, k_words, k_scales, nb, offs, out):
     nc = tc.nc
     with ExitStack() as ctx:
         sb = ctx.enter_context(tc.tile_pool(name="sb", bufs=1))
-        early = ctx.enter_context(tc.tile_pool(name="early", bufs=1))
+        shared = ctx.enter_context(tc.tile_pool(name="shared", bufs=1))
         ps = ctx.enter_context(tc.psum_pool(name="ps", bufs=1))
 
         offsets = sb.tile([P, N // 16], U16, name="offsets")
         q_raw = sb.tile([P, PACK, NQ], F32, name="q_raw")
-        scale_win = sb.tile([P, T], U8, name="scale_win", align_bytes=64)
+        scale_win = sb.tile([P, T + 4], U8, name="scale_win", align_bytes=64)
         word_win = sb.tile([P, T], U32, name="word_win", align_bytes=64)
-        nb_win = sb.tile([P, T], F32, name="nb_win")
+        nb_win = shared.tile([P, T + 1], F32, name="nb_win", offset=0, align_bytes=64)
         ident = sb.tile([P, P], F32, name="ident")
         k_sc = sb.tile([P, N], U8, name="k_sc", align_bytes=64)
-        zeros = early.tile([P, 3 * P], F32, name="zeros", offset=1984, align_bytes=64)
+        zeros = sb.tile([P, P], F32, name="zeros")
+        win_v = sb.tile([P, T], F32, name="win_v")
         live = P - 1
 
-        def half_list(h):
-            return offsets[:, h * (HALF // 16) : (h + 1) * (HALF // 16)]
+        def part(lo, hi):
+            return offsets[:, lo // 16 : hi // 16]
 
-        nc.vector.memset(scale_win[0:ROW0, :].bitcast(I32), 0)
-        nc.vector.memset(scale_win[ROW0 + 16 : P, :].bitcast(I32), 0)
-        nc.vector.memset(k_sc[:].bitcast(I32), 0)
-        nc.vector.memset(nb_win[0:live, :].bitcast(I32), 0)
-        nc.vector.memset(zeros[:, 0:P], 0.0)
+        nc.gpsimd.memset(zeros[:], 0.0)
+        nc.gpsimd.memset(nb_win[0:live, 0:POOL_NB].bitcast(I32), 0)
+        nc.gpsimd.memset(k_sc[:].bitcast(I32), 0)
         nc.gpsimd.affine_select(
             out=ident[:],
-            in_=zeros[:, 0:P],
+            in_=zeros[:],
             compare_op=ALU.not_equal,
             fill=1.0,
             base=0,
             pattern=[[-1, P]],
             channel_multiplier=1,
         )
-        out_win = early.tile([P, T], F32, name="out_win", offset=3456, align_bytes=64)
-        nc.gpsimd.memset(out_win[:, 0 : T - LATE].bitcast(I32), 0)
+        warm = sb.tile([P, 1], F32, name="warm")
+        nc.scalar.activation(warm[:], zeros[:, 0:1], ACT.Copy)
+        nc.vector.memset(nb_win[0:live, POOL_NB : T + 1].bitcast(I32), 0)
+        nc.vector.memset(scale_win[0:ROW0, :].bitcast(I32), 0)
+        nc.vector.memset(scale_win[ROW0 + 16 : P, :].bitcast(I32), 0)
 
-        nc.sync.dma_start(scale_win[ROW0 : ROW0 + 16, :].bitcast(I32), k_scales[0].bitcast(I32))
-        nc.scalar.dma_start(nb_win[live:P, :], nb[0:1, :])
+        nc.sync.dma_start(scale_win[ROW0 : ROW0 + 16, 0:T].bitcast(I32), k_scales[0].bitcast(I32))
+        nc.scalar.dma_start(nb_win[live:P, 0:T], nb[0:1, :])
         nc.sync.dma_start(offsets[:], offs)
         nc.sync.dma_start(q_raw[:], qT[0].rearrange("(p j) w -> p j w", j=PACK))
         nc.sync.dma_start(word_win[:].bitcast(I32), k_words[0].rearrange("p n t -> p (n t)").bitcast(I32))
 
-        q_bf = sb.tile([P, NQ, PACK], BF16, name="q_bf", align_bytes=64)
+        picked = sb.tile([P, N], U8, name="picked", align_bytes=64)
+        nc.vector.tensor_copy(picked[:], scale_win[:, 0:T].indirect(offsets[:]))
+        for a in range(4):
+            nc.sync.dma_start(
+                k_sc[32 * a : 32 * a + 4, :].bitcast(I32),
+                picked[ROW0 + 4 * a : ROW0 + 4 * a + 4, :].bitcast(I32),
+            )
+
+        nb_row = sb.tile([P, N], F32, name="nb_row")
+        nc.scalar.activation(nb_row[:], nb_win[:, 0:T].indirect(offsets[:]), ACT.Copy)
+
+        nc.gpsimd.memset(win_v[:].bitcast(I32), 0)
+
+        q_bf = shared.tile([P, NQ, PACK], BF16, name="q_bf", offset=4 * T - 512, align_bytes=64)
         nc.scalar.copy(q_bf[:], q_raw[:].rearrange("p j w -> p w j"))
-
-        def pick_scales(h, picked):
-            nc.vector.tensor_copy(picked[:], scale_win[:].indirect(half_list(h)))
-            for a in range(4):
-                nc.sync.dma_start(
-                    k_sc[32 * a : 32 * a + 4, h * HALF : (h + 1) * HALF].bitcast(I32),
-                    picked[ROW0 + 4 * a : ROW0 + 4 * a + 4, :].bitcast(I32),
-                )
-
-        picked0 = sb.tile([P, HALF], U8, name="picked0", align_bytes=64)
-        pick_scales(0, picked0)
-        nb_row0 = sb.tile([P, HALF], F32, name="nb_row0")
-        nc.vector.tensor_copy(nb_row0[:], nb_win[:].indirect(half_list(0)))
-        picked1 = early.tile([P, HALF], U8, name="picked1", offset=3200, align_bytes=64)
-        pick_scales(1, picked1)
-
-        nb_row1 = early.tile([P, HALF], F32, name="nb_row1", offset=2048, align_bytes=64)
-        nc.vector.tensor_copy(nb_row1[:], nb_win[:].indirect(half_list(1)))
-        nb_rows = [nb_row0, nb_row1]
-
         q_codes = sb.tile([P, NQ], U32, name="q_codes", align_bytes=64)
-        q_sc = early.tile([P, NQ], U8, name="q_sc", offset=3072, align_bytes=64)
+        q_sc = sb.tile([P, NQ], U8, name="q_sc", align_bytes=64)
         nc.vector.quantize_mx(out=q_codes[:].bitcast(FP8X4), scales=q_sc[:], in_=q_bf[:].rearrange("p w j -> p (w j)"))
 
-        bias = sb.tile([P, HALF], F32, name="bias")
-        cols0 = []
-        for c in range(2):
-            turned = ps.tile([P, (P, 4 * 512)[c]], F32, name=f"turned0_{c}", offset=(7 * BANK, 0)[c])
-            nc.tensor.transpose(turned[:, 0:P], nb_rows[0][:, c * P : (c + 1) * P], ident[:])
-            nb_col = sb.tile([P, 1], F32, name=f"nb_col0_{c}")
-            nc.scalar.copy(nb_col[:], turned[:, live:P])
-            cols0.append(nb_col)
-        for c in range(2):
-            spread = ps.tile([P, P], F32, name=f"spread{c}", offset=(4 + c) * BANK)
-            nc.tensor.transpose(spread[:], cols0[c][:].to_broadcast([P, P]), ident[:])
-            nc.scalar.copy(bias[:, c * P : (c + 1) * P], spread[:])
-        turned1 = ps.tile([P, 2, P], F32, name="turned1", offset=2 * BANK)
-        for c in range(2):
-            nc.tensor.transpose(turned1[:, c, :], nb_rows[1][:, c * P : (c + 1) * P], ident[:])
-        col1 = sb.tile([P, 2], F32, name="col1")
-        nc.scalar.copy(col1[:], turned1[:, :, live])
+        win_s = shared.tile([P, T], F32, name="win_s", offset=0, align_bytes=64)
+        nc.gpsimd.memset(win_s[:].bitcast(I32), 0)
 
-        k_all = early.tile([P, N], U32, name="k_all", offset=0, align_bytes=64)
-        k_codes = [k_all[:, 0:HALF], k_all[:, HALF:N]]
+        turned = ps.tile([P, 8, P], F32, name="turned", offset=0)
+        for c in range(4):
+            nc.tensor.transpose(turned[:, c, :], nb_row[:, c * P : (c + 1) * P], ident[:])
+        nb_col = sb.tile([P, 4], F32, name="nb_col")
+        nc.scalar.copy(nb_col[:], turned[:, 0:4, live])
+        bias = sb.tile([P, N], F32, name="bias")
+        spread = ps.tile([P, 4, P], F32, name="spread", offset=2 * BANK)
+        for c in range(4):
+            nc.tensor.transpose(spread[:, c, :], nb_col[:, c : c + 1].to_broadcast([P, P]), ident[:])
+        nc.scalar.copy(bias[:], spread[:].rearrange("p c w -> p (c w)"))
+
+        k_codes = shared.tile([P, N], U32, name="k_codes", offset=4 * T + 64, align_bytes=64)
+        acc = []
         for h in range(2):
-            nc.vector.tensor_copy(k_codes[h], word_win[:].indirect(half_list(h)))
-        nc.vector.memset(out_win[:, T - LATE : T].bitcast(I32), 0)
-
-        floor = sb.tile([P, HALF], F32, name="floor")
-        for c in range(2):
-            cols = slice(c * P, (c + 1) * P)
-            a = ps.tile([P, P], F32, name=f"acc{c}", offset=c * BANK)
+            cols = slice(h * HALF, (h + 1) * HALF)
+            nc.vector.tensor_copy(k_codes[:, cols], word_win[:].indirect(part(h * HALF, (h + 1) * HALF)))
+            a = ps.tile([P, HALF], F32, name=f"acc{h}", offset=h * BANK)
             nc.tensor.matmul_mx(
                 out=a[:],
                 lhsT=q_codes[:].bitcast(FP8X4),
                 lhsT_scale=q_sc[:],
-                rhs=k_codes[0][:, cols].bitcast(FP8X4),
+                rhs=k_codes[:, cols].bitcast(FP8X4),
                 rhs_scale=k_sc[:, cols],
                 start=True,
                 stop=True,
             )
-            nc.vector.scalar_tensor_tensor(floor[:, cols], bias[:, cols], -1.0, a[:], ALU.mult, ALU.max)
+            acc.append(a)
 
-        by_slot = []
-        for c in range(2):
-            b = ps.tile([P, P], F32, name=f"by_slot{c}", offset=(3, 5)[c] * BANK)
-            nc.tensor.matmul_mx(
-                out=b[:],
-                lhsT=k_codes[1][:, c * P : (c + 1) * P].bitcast(FP8X4),
-                lhsT_scale=k_sc[:, HALF + c * P : HALF + (c + 1) * P],
-                rhs=q_codes[:].bitcast(FP8X4),
-                rhs_scale=q_sc[:],
-                start=True,
-                stop=True,
-            )
-            by_slot.append(b)
-        y_slot = sb.tile([P, 2, P], F32, name="y_slot")
-        y = sb.tile([P, HALF], F32, name="y")
-        for c in range(2):
-            nc.scalar.activation(y_slot[:, c, :], by_slot[c][:], ACT.Relu, bias=col1[:, c : c + 1])
-        for c in range(2):
-            by_query = ps.tile([P, P], F32, name=f"by_query{c}", offset=(6 + c) * BANK)
-            nc.tensor.transpose(by_query[:], y_slot[:, c, :], ident[:])
-            nc.scalar.copy(y[:, c * P : (c + 1) * P], by_query[:])
+        raw_v = sb.tile([P, HALF], F32, name="raw_v")
+        nc.scalar.copy(raw_v[:], acc[0][:])
+        sum_s = sb.tile([P, HALF], F32, name="sum_s")
+        nc.vector.tensor_tensor(sum_s[:], acc[1][:], bias[:, HALF:N], ALU.add)
+        nc.vector.tensor_tensor(win_v[:].indirect(part(0, HALF)), raw_v[:], bias[:, 0:HALF], ALU.add)
+        nc.scalar.activation(win_s[:].indirect(part(HALF, N)), sum_s[:], ACT.Copy)
 
-        nc.vector.tensor_tensor(out_win[:].indirect(half_list(0)), floor[:], bias[:], ALU.add)
-        nc.vector.tensor_copy(out_win[:].indirect(half_list(1)), y[:])
-
-        nc.sync.dma_start(out[0], out_win[:])
+        result = sb.tile([P, T], F32, name="result")
+        for c in range(T // CHUNK):
+            cols = slice(c * CHUNK, (c + 1) * CHUNK)
+            nc.vector.tensor_tensor(result[:, cols], win_v[:, cols], win_s[:, cols], ALU.max)
+            nc.sync.dma_start(out[0][:, cols], result[:, cols])

@@ -9,10 +9,11 @@ D = 512
 NQ = 128
 PACK = 4
 HALF = N // 2
-ROW0 = 48
 BANK = 2048
-POOL_NB = 1048
-CHUNK = 256
+ROW0 = 48
+POOL_NB = 1552
+PIECES = (0, 256, 384, 512)
+CHUNKS = (0, 256, 640, 1088, 1536, 2048)
 
 FLOPS = 2 * D * NQ * N
 
@@ -38,11 +39,11 @@ def tile_attend_neu_scat_topk_kernel(tc, qT, k_words, k_scales, nb, offs, out):
         q_raw = sb.tile([P, PACK, NQ], F32, name="q_raw")
         scale_win = sb.tile([P, T + 4], U8, name="scale_win", align_bytes=64)
         word_win = sb.tile([P, T], U32, name="word_win", align_bytes=64)
-        nb_win = shared.tile([P, T + 1], F32, name="nb_win", offset=0, align_bytes=64)
+        nb_win = sb.tile([P, T + 1], F32, name="nb_win")
         ident = sb.tile([P, P], F32, name="ident")
-        k_sc = sb.tile([P, N], U8, name="k_sc", align_bytes=64)
+        k_sc = sb.tile([P, N + 4], U8, name="k_sc", align_bytes=64)
         zeros = sb.tile([P, P], F32, name="zeros")
-        win_v = sb.tile([P, T], F32, name="win_v")
+        win_s = sb.tile([P, T], F32, name="win_s")
         live = P - 1
 
         def part(lo, hi):
@@ -50,7 +51,6 @@ def tile_attend_neu_scat_topk_kernel(tc, qT, k_words, k_scales, nb, offs, out):
 
         nc.gpsimd.memset(zeros[:], 0.0)
         nc.gpsimd.memset(nb_win[0:live, 0:POOL_NB].bitcast(I32), 0)
-        nc.gpsimd.memset(k_sc[:].bitcast(I32), 0)
         nc.gpsimd.affine_select(
             out=ident[:],
             in_=zeros[:],
@@ -60,11 +60,13 @@ def tile_attend_neu_scat_topk_kernel(tc, qT, k_words, k_scales, nb, offs, out):
             pattern=[[-1, P]],
             channel_multiplier=1,
         )
+        nc.gpsimd.memset(win_s[:].bitcast(I32), 0)
         warm = sb.tile([P, 1], F32, name="warm")
         nc.scalar.activation(warm[:], zeros[:, 0:1], ACT.Copy)
-        nc.vector.memset(nb_win[0:live, POOL_NB : T + 1].bitcast(I32), 0)
         nc.vector.memset(scale_win[0:ROW0, :].bitcast(I32), 0)
         nc.vector.memset(scale_win[ROW0 + 16 : P, :].bitcast(I32), 0)
+        nc.vector.memset(k_sc[:].bitcast(I32), 0)
+        nc.vector.memset(nb_win[0:live, POOL_NB : T + 1].bitcast(I32), 0)
 
         nc.sync.dma_start(scale_win[ROW0 : ROW0 + 16, 0:T].bitcast(I32), k_scales[0].bitcast(I32))
         nc.scalar.dma_start(nb_win[live:P, 0:T], nb[0:1, :])
@@ -72,45 +74,58 @@ def tile_attend_neu_scat_topk_kernel(tc, qT, k_words, k_scales, nb, offs, out):
         nc.sync.dma_start(q_raw[:], qT[0].rearrange("(p j) w -> p j w", j=PACK))
         nc.sync.dma_start(word_win[:].bitcast(I32), k_words[0].rearrange("p n t -> p (n t)").bitcast(I32))
 
+        halves = [slice(0, HALF), slice(HALF, N)]
         picked = sb.tile([P, N], U8, name="picked", align_bytes=64)
-        nc.vector.tensor_copy(picked[:], scale_win[:, 0:T].indirect(offsets[:]))
-        for a in range(4):
+
+        def lay(a, cols):
             nc.sync.dma_start(
-                k_sc[32 * a : 32 * a + 4, :].bitcast(I32),
-                picked[ROW0 + 4 * a : ROW0 + 4 * a + 4, :].bitcast(I32),
+                k_sc[32 * a : 32 * a + 4, cols].bitcast(I32),
+                picked[ROW0 + 4 * a : ROW0 + 4 * a + 4, cols].bitcast(I32),
             )
 
-        nb_row = sb.tile([P, N], F32, name="nb_row")
-        nc.scalar.activation(nb_row[:], nb_win[:, 0:T].indirect(offsets[:]), ACT.Copy)
+        nc.vector.tensor_copy(picked[:, halves[0]], scale_win[:, 0:T].indirect(part(0, HALF)))
+        for a in range(3):
+            lay(a, halves[0])
+        nc.vector.tensor_copy(picked[:, halves[1]], scale_win[:, 0:T].indirect(part(HALF, N)))
+        lay(3, slice(0, N))
+        for a in range(3):
+            lay(a, halves[1])
 
-        nc.gpsimd.memset(win_v[:].bitcast(I32), 0)
+        nb_row = sb.tile([P, N], F32, name="nb_row")
+        for cols in halves:
+            nc.scalar.activation(nb_row[:, cols], nb_win[:, 0:T].indirect(part(cols.start, cols.stop)), ACT.Copy)
 
         q_bf = shared.tile([P, NQ, PACK], BF16, name="q_bf", offset=4 * T - 512, align_bytes=64)
-        nc.scalar.copy(q_bf[:], q_raw[:].rearrange("p j w -> p w j"))
+        for rows in (slice(0, 63), slice(63, NQ)):
+            nc.vector.tensor_copy(q_bf[:, rows, :], q_raw[:, :, rows].rearrange("p j w -> p w j"))
         q_codes = sb.tile([P, NQ], U32, name="q_codes", align_bytes=64)
         q_sc = sb.tile([P, NQ], U8, name="q_sc", align_bytes=64)
         nc.vector.quantize_mx(out=q_codes[:].bitcast(FP8X4), scales=q_sc[:], in_=q_bf[:].rearrange("p w j -> p (w j)"))
 
-        win_s = shared.tile([P, T], F32, name="win_s", offset=0, align_bytes=64)
-        nc.gpsimd.memset(win_s[:].bitcast(I32), 0)
+        win_v = shared.tile([P, T], F32, name="win_v", offset=0, align_bytes=64)
+        nc.gpsimd.memset(win_v[:].bitcast(I32), 0)
 
-        turned = ps.tile([P, 8, P], F32, name="turned", offset=0)
-        for c in range(4):
-            nc.tensor.transpose(turned[:, c, :], nb_row[:, c * P : (c + 1) * P], ident[:])
-        nb_col = sb.tile([P, 4], F32, name="nb_col")
-        nc.scalar.copy(nb_col[:], turned[:, 0:4, live])
         bias = sb.tile([P, N], F32, name="bias")
-        spread = ps.tile([P, 4, P], F32, name="spread", offset=2 * BANK)
-        for c in range(4):
-            nc.tensor.transpose(spread[:, c, :], nb_col[:, c : c + 1].to_broadcast([P, P]), ident[:])
-        nc.scalar.copy(bias[:], spread[:].rearrange("p c w -> p (c w)"))
-
-        k_codes = shared.tile([P, N], U32, name="k_codes", offset=4 * T + 64, align_bytes=64)
-        acc = []
+        nb_col = []
         for h in range(2):
-            cols = slice(h * HALF, (h + 1) * HALF)
-            nc.vector.tensor_copy(k_codes[:, cols], word_win[:].indirect(part(h * HALF, (h + 1) * HALF)))
-            a = ps.tile([P, HALF], F32, name=f"acc{h}", offset=h * BANK)
+            turned = ps.tile([P, (4, 16)[h], P], F32, name=f"turned{h}", offset=h * BANK)
+            for c in range(2):
+                nc.tensor.transpose(turned[:, c, :], nb_row[:, (2 * h + c) * P : (2 * h + c + 1) * P], ident[:])
+            col = sb.tile([P, 2], F32, name=f"nb_col{h}")
+            nc.scalar.copy(col[:], turned[:, 0:2, live])
+            nb_col.append(col)
+        for h in range(2):
+            spread = ps.tile([P, 2, P], F32, name=f"spread{h}", offset=(5 + h) * BANK)
+            for c in range(2):
+                nc.tensor.transpose(spread[:, c, :], nb_col[h][:, c : c + 1].to_broadcast([P, P]), ident[:])
+            nc.scalar.copy(bias[:, halves[h]], spread[:].rearrange("p c w -> p (c w)"))
+
+        k_codes = shared.tile([P, N], U32, name="k_codes", offset=4 * T, align_bytes=64)
+        acc = []
+        pieces = [slice(lo, hi) for lo, hi in zip(PIECES, PIECES[1:])]
+        for h, cols in enumerate(pieces):
+            nc.vector.tensor_copy(k_codes[:, cols], word_win[:].indirect(part(cols.start, cols.stop)))
+            a = ps.tile([P, cols.stop - cols.start], F32, name=f"acc{h}", offset=(2 + h) * BANK)
             nc.tensor.matmul_mx(
                 out=a[:],
                 lhsT=q_codes[:].bitcast(FP8X4),
@@ -122,15 +137,14 @@ def tile_attend_neu_scat_topk_kernel(tc, qT, k_words, k_scales, nb, offs, out):
             )
             acc.append(a)
 
-        raw_v = sb.tile([P, HALF], F32, name="raw_v")
-        nc.scalar.copy(raw_v[:], acc[0][:])
-        sum_s = sb.tile([P, HALF], F32, name="sum_s")
-        nc.vector.tensor_tensor(sum_s[:], acc[1][:], bias[:, HALF:N], ALU.add)
-        nc.vector.tensor_tensor(win_v[:].indirect(part(0, HALF)), raw_v[:], bias[:, 0:HALF], ALU.add)
-        nc.scalar.activation(win_s[:].indirect(part(HALF, N)), sum_s[:], ACT.Copy)
+        sums = sb.tile([P, N], F32, name="sums")
+        for h, cols in enumerate(pieces):
+            nc.vector.tensor_tensor(sums[:, cols], acc[h][:], bias[:, cols], ALU.add)
+        nc.scalar.activation(win_s[:].indirect(part(0, HALF)), sums[:, halves[0]], ACT.Copy)
+        nc.vector.tensor_copy(win_v[:].indirect(part(HALF, N)), sums[:, halves[1]])
 
         result = sb.tile([P, T], F32, name="result")
-        for c in range(T // CHUNK):
-            cols = slice(c * CHUNK, (c + 1) * CHUNK)
+        for lo, hi in zip(CHUNKS, CHUNKS[1:]):
+            cols = slice(lo, hi)
             nc.vector.tensor_tensor(result[:, cols], win_v[:, cols], win_s[:, cols], ALU.max)
             nc.sync.dma_start(out[0][:, cols], result[:, cols])

@@ -11,7 +11,8 @@ PACK = 4
 HALF = N // 2
 BANK = 2048
 ROW0 = 48
-POOL_NB = 1552
+POOL_NB = 1344
+POOL_WIN = 1696
 PIECES = (0, 256, 384, 512)
 CHUNKS = (0, 256, 640, 1088, 1536, 2048)
 
@@ -42,31 +43,21 @@ def tile_attend_neu_scat_topk_kernel(tc, qT, k_words, k_scales, nb, offs, out):
         nb_win = sb.tile([P, T + 1], F32, name="nb_win")
         ident = sb.tile([P, P], F32, name="ident")
         k_sc = sb.tile([P, N + 4], U8, name="k_sc", align_bytes=64)
-        zeros = sb.tile([P, P], F32, name="zeros")
+        gap = sb.tile([P, P], I32, name="gap")
         win_s = sb.tile([P, T], F32, name="win_s")
         live = P - 1
 
         def part(lo, hi):
             return offsets[:, lo // 16 : hi // 16]
 
-        nc.gpsimd.memset(zeros[:], 0.0)
+        nc.gpsimd.iota(gap[:], pattern=[[1, P]], base=0, channel_multiplier=-1)
+        nc.scalar.activation(ident[:], gap[:].bitcast(U32), ACT.Relu, bias=1.0, scale=-1.0)
         nc.gpsimd.memset(nb_win[0:live, 0:POOL_NB].bitcast(I32), 0)
-        nc.gpsimd.affine_select(
-            out=ident[:],
-            in_=zeros[:],
-            compare_op=ALU.not_equal,
-            fill=1.0,
-            base=0,
-            pattern=[[-1, P]],
-            channel_multiplier=1,
-        )
-        nc.gpsimd.memset(win_s[:].bitcast(I32), 0)
-        warm = sb.tile([P, 1], F32, name="warm")
-        nc.scalar.activation(warm[:], zeros[:, 0:1], ACT.Copy)
+        nc.gpsimd.memset(win_s[:, 0:POOL_WIN].bitcast(I32), 0)
+        nc.vector.memset(nb_win[0:live, POOL_NB : T + 1].bitcast(I32), 0)
         nc.vector.memset(scale_win[0:ROW0, :].bitcast(I32), 0)
         nc.vector.memset(scale_win[ROW0 + 16 : P, :].bitcast(I32), 0)
         nc.vector.memset(k_sc[:].bitcast(I32), 0)
-        nc.vector.memset(nb_win[0:live, POOL_NB : T + 1].bitcast(I32), 0)
 
         nc.sync.dma_start(scale_win[ROW0 : ROW0 + 16, 0:T].bitcast(I32), k_scales[0].bitcast(I32))
         nc.scalar.dma_start(nb_win[live:P, 0:T], nb[0:1, :])
@@ -92,12 +83,13 @@ def tile_attend_neu_scat_topk_kernel(tc, qT, k_words, k_scales, nb, offs, out):
             lay(a, halves[1])
 
         nb_row = sb.tile([P, N], F32, name="nb_row")
-        for cols in halves:
-            nc.scalar.activation(nb_row[:, cols], nb_win[:, 0:T].indirect(part(cols.start, cols.stop)), ACT.Copy)
+        nc.scalar.activation(nb_row[:, halves[0]], nb_win[:, 0:T].indirect(part(0, HALF)), ACT.Copy)
+        nc.scalar.activation(nb_row[:, halves[1]], nb_win[:, 0:T].indirect(part(HALF, N)), ACT.Copy)
+        nc.vector.memset(win_s[:, POOL_WIN : T - 1].bitcast(I32), 0)
+        nc.vector.memset(win_s[:, T - 1 : T].bitcast(I32), 0)
 
         q_bf = shared.tile([P, NQ, PACK], BF16, name="q_bf", offset=4 * T - 512, align_bytes=64)
-        for rows in (slice(0, 63), slice(63, NQ)):
-            nc.vector.tensor_copy(q_bf[:, rows, :], q_raw[:, :, rows].rearrange("p j w -> p w j"))
+        nc.vector.tensor_copy(q_bf[:], q_raw[:].rearrange("p j w -> p w j"))
         q_codes = sb.tile([P, NQ], U32, name="q_codes", align_bytes=64)
         q_sc = sb.tile([P, NQ], U8, name="q_sc", align_bytes=64)
         nc.vector.quantize_mx(out=q_codes[:].bitcast(FP8X4), scales=q_sc[:], in_=q_bf[:].rearrange("p w j -> p (w j)"))

@@ -12,9 +12,8 @@ HALF = N // 2
 BANK = 2048
 ROW0 = 48
 POOL_NB = 1344
-POOL_WIN = 1696
 PIECES = (0, 256, 384, 512)
-CHUNKS = (0, 256, 640, 1088, 1536, 2048)
+CHUNKS = (0, 256, 512, 1024, 1536, 2048)
 
 FLOPS = 2 * D * NQ * N
 
@@ -53,7 +52,7 @@ def tile_attend_neu_scat_topk_kernel(tc, qT, k_words, k_scales, nb, offs, out):
         nc.gpsimd.iota(gap[:], pattern=[[1, P]], base=0, channel_multiplier=-1)
         nc.scalar.activation(ident[:], gap[:].bitcast(U32), ACT.Relu, bias=1.0, scale=-1.0)
         nc.gpsimd.memset(nb_win[0:live, 0:POOL_NB].bitcast(I32), 0)
-        nc.gpsimd.memset(win_s[:, 0:POOL_WIN].bitcast(I32), 0)
+        nc.gpsimd.memset(win_s[:].bitcast(I32), 0)
         nc.vector.memset(nb_win[0:live, POOL_NB : T + 1].bitcast(I32), 0)
         nc.vector.memset(scale_win[0:ROW0, :].bitcast(I32), 0)
         nc.vector.memset(scale_win[ROW0 + 16 : P, :].bitcast(I32), 0)
@@ -85,11 +84,10 @@ def tile_attend_neu_scat_topk_kernel(tc, qT, k_words, k_scales, nb, offs, out):
         nb_row = sb.tile([P, N], F32, name="nb_row")
         nc.scalar.activation(nb_row[:, halves[0]], nb_win[:, 0:T].indirect(part(0, HALF)), ACT.Copy)
         nc.scalar.activation(nb_row[:, halves[1]], nb_win[:, 0:T].indirect(part(HALF, N)), ACT.Copy)
-        nc.vector.memset(win_s[:, POOL_WIN : T - 1].bitcast(I32), 0)
-        nc.vector.memset(win_s[:, T - 1 : T].bitcast(I32), 0)
 
         q_bf = shared.tile([P, NQ, PACK], BF16, name="q_bf", offset=4 * T - 512, align_bytes=64)
-        nc.vector.tensor_copy(q_bf[:], q_raw[:].rearrange("p j w -> p w j"))
+        for rows in (slice(0, 63), slice(63, NQ)):
+            nc.vector.tensor_copy(q_bf[:, rows, :], q_raw[:, :, rows].rearrange("p j w -> p w j"))
         q_codes = sb.tile([P, NQ], U32, name="q_codes", align_bytes=64)
         q_sc = sb.tile([P, NQ], U8, name="q_sc", align_bytes=64)
         nc.vector.quantize_mx(out=q_codes[:].bitcast(FP8X4), scales=q_sc[:], in_=q_bf[:].rearrange("p w j -> p (w j)"))

@@ -11,9 +11,9 @@ PACK = 4
 HALF = N // 2
 BANK = 2048
 ROW0 = 48
-POOL_NB = 1344
+POOL_NB = 1600
 PIECES = (0, 256, 384, 512)
-CHUNKS = (0, 256, 512, 1024, 1536, 2048)
+CHUNKS = (0, 256, 672, 1280, 2048)
 
 FLOPS = 2 * D * NQ * N
 
@@ -53,10 +53,10 @@ def tile_attend_neu_scat_topk_kernel(tc, qT, k_words, k_scales, nb, offs, out):
         nc.scalar.activation(ident[:], gap[:].bitcast(U32), ACT.Relu, bias=1.0, scale=-1.0)
         nc.gpsimd.memset(nb_win[0:live, 0:POOL_NB].bitcast(I32), 0)
         nc.gpsimd.memset(win_s[:].bitcast(I32), 0)
-        nc.vector.memset(nb_win[0:live, POOL_NB : T + 1].bitcast(I32), 0)
         nc.vector.memset(scale_win[0:ROW0, :].bitcast(I32), 0)
         nc.vector.memset(scale_win[ROW0 + 16 : P, :].bitcast(I32), 0)
         nc.vector.memset(k_sc[:].bitcast(I32), 0)
+        nc.vector.memset(nb_win[0:live, POOL_NB : T + 1].bitcast(I32), 0)
 
         nc.sync.dma_start(scale_win[ROW0 : ROW0 + 16, 0:T].bitcast(I32), k_scales[0].bitcast(I32))
         nc.scalar.dma_start(nb_win[live:P, 0:T], nb[0:1, :])

@@ -13,7 +13,7 @@ BANK = 2048
 ROW0 = 48
 POOL_NB = 1600
 PIECES = (0, 256, 384, 512)
-CHUNKS = (0, 256, 672, 1280, 2048)
+CHUNKS = (0, 416, 896, 1440, 2048)
 
 FLOPS = 2 * D * NQ * N
 

@@ -128,10 +128,11 @@ def tile_attend_neu_scat_topk_kernel(tc, qT, k_words, k_scales, nb, offs, out):
             acc.append(a)
 
         sums = sb.tile([P, N], F32, name="sums")
-        for h, cols in enumerate(pieces):
-            nc.vector.tensor_tensor(sums[:, cols], acc[h][:], bias[:, cols], ALU.add)
+        nc.vector.tensor_tensor(sums[:, pieces[0]], acc[0][:], bias[:, pieces[0]], ALU.add)
+        for h in (1, 2):
+            nc.scalar.copy(sums[:, pieces[h]], acc[h][:])
         nc.scalar.activation(win_s[:].indirect(part(0, HALF)), sums[:, halves[0]], ACT.Copy)
-        nc.vector.tensor_copy(win_v[:].indirect(part(HALF, N)), sums[:, halves[1]])
+        nc.vector.tensor_tensor(win_v[:].indirect(part(HALF, N)), sums[:, halves[1]], bias[:, halves[1]], ALU.add)
 
         result = sb.tile([P, T], F32, name="result")
         for lo, hi in zip(CHUNKS, CHUNKS[1:]):

@@ -10,6 +10,7 @@ NQ = 128
 PACK = 4
 HALF = N // 2
 BANK = 2048
+LINE = 256
 ROW0 = 48
 POOL_NB = 1600
 PIECES = (0, 256, 384, 512)
@@ -36,10 +37,10 @@ def tile_attend_neu_scat_topk_kernel(tc, qT, k_words, k_scales, nb, offs, out):
         ps = ctx.enter_context(tc.psum_pool(name="ps", bufs=1))
 
         offsets = sb.tile([P, N // 16], U16, name="offsets")
-        q_raw = sb.tile([P, PACK, NQ], F32, name="q_raw")
-        scale_win = sb.tile([P, T + 4], U8, name="scale_win", align_bytes=64)
-        word_win = sb.tile([P, T], U32, name="word_win", align_bytes=64)
-        nb_win = sb.tile([P, T + 1], F32, name="nb_win")
+        q_raw = sb.tile([P, PACK, NQ], F32, name="q_raw", align_bytes=LINE)
+        scale_win = sb.tile([P, T + 4], U8, name="scale_win", align_bytes=LINE)
+        word_win = sb.tile([P, T], U32, name="word_win", align_bytes=LINE)
+        nb_win = sb.tile([P, T + 1], F32, name="nb_win", align_bytes=LINE)
         ident = sb.tile([P, P], F32, name="ident")
         k_sc = sb.tile([P, N + 4], U8, name="k_sc", align_bytes=64)
         gap = sb.tile([P, P], I32, name="gap")
@@ -134,7 +135,7 @@ def tile_attend_neu_scat_topk_kernel(tc, qT, k_words, k_scales, nb, offs, out):
         nc.scalar.activation(win_s[:].indirect(part(0, HALF)), sums[:, halves[0]], ACT.Copy)
         nc.vector.tensor_tensor(win_v[:].indirect(part(HALF, N)), sums[:, halves[1]], bias[:, halves[1]], ALU.add)
 
-        result = sb.tile([P, T], F32, name="result")
+        result = sb.tile([P, T], F32, name="result", align_bytes=LINE)
         for lo, hi in zip(CHUNKS, CHUNKS[1:]):
             cols = slice(lo, hi)
             nc.vector.tensor_tensor(result[:, cols], win_v[:, cols], win_s[:, cols], ALU.max)

@@ -14,7 +14,7 @@ LINE = 256
 ROW0 = 48
 POOL_NB = 1600
 PIECES = (0, 256, 384, 512)
-CHUNKS = (0, 416, 896, 1440, 2048)
+CHUNKS = (0, 384, 896, 1472, 2048)
 
 FLOPS = 2 * D * NQ * N
 

@@ -12,7 +12,7 @@ HALF = N // 2
 BANK = 2048
 LINE = 256
 ROW0 = 48
-POOL_NB = 1600
+POOL_NB = 1696
 PIECES = (0, 256, 384, 512)
 CHUNKS = (0, 384, 896, 1472, 2048)
 
@@ -59,9 +59,9 @@ def tile_attend_neu_scat_topk_kernel(tc, qT, k_words, k_scales, nb, offs, out):
         nc.vector.memset(k_sc[:].bitcast(I32), 0)
         nc.vector.memset(nb_win[0:live, POOL_NB : T + 1].bitcast(I32), 0)
 
-        nc.sync.dma_start(scale_win[ROW0 : ROW0 + 16, 0:T].bitcast(I32), k_scales[0].bitcast(I32))
-        nc.scalar.dma_start(nb_win[live:P, 0:T], nb[0:1, :])
+        nc.scalar.dma_start(scale_win[ROW0 : ROW0 + 16, 0:T].bitcast(I32), k_scales[0].bitcast(I32))
         nc.sync.dma_start(offsets[:], offs)
+        nc.sync.dma_start(nb_win[live:P, 0:T], nb[0:1, :])
         nc.sync.dma_start(q_raw[:], qT[0].rearrange("(p j) w -> p j w", j=PACK))
         nc.sync.dma_start(word_win[:].bitcast(I32), k_words[0].rearrange("p n t -> p (n t)").bitcast(I32))
 

@@ -10,6 +10,7 @@ NQ = 128
 PACK = 4
 HALF = N // 2
 BANK = 2048
+CUT = 288
 LINE = 256
 ROW0 = 48
 POOL_NB = 1696
@@ -129,11 +130,13 @@ def tile_attend_neu_scat_topk_kernel(tc, qT, k_words, k_scales, nb, offs, out):
             acc.append(a)
 
         sums = sb.tile([P, N], F32, name="sums")
+        extra = CUT - HALF
         nc.vector.tensor_tensor(sums[:, pieces[0]], acc[0][:], bias[:, pieces[0]], ALU.add)
-        for h in (1, 2):
-            nc.scalar.copy(sums[:, pieces[h]], acc[h][:])
-        nc.scalar.activation(win_s[:].indirect(part(0, HALF)), sums[:, halves[0]], ACT.Copy)
-        nc.vector.tensor_tensor(win_v[:].indirect(part(HALF, N)), sums[:, halves[1]], bias[:, halves[1]], ALU.add)
+        nc.vector.tensor_tensor(sums[:, HALF:CUT], acc[1][:, 0:extra], bias[:, HALF:CUT], ALU.add)
+        nc.vector.tensor_copy(sums[:, CUT : PIECES[2]], acc[1][:, extra:P])
+        nc.scalar.copy(sums[:, pieces[2]], acc[2][:])
+        nc.scalar.activation(win_s[:].indirect(part(0, CUT)), sums[:, 0:CUT], ACT.Copy)
+        nc.vector.tensor_tensor(win_v[:].indirect(part(CUT, N)), sums[:, CUT:N], bias[:, CUT:N], ALU.add)
 
         result = sb.tile([P, T], F32, name="result", align_bytes=LINE)
         for lo, hi in zip(CHUNKS, CHUNKS[1:]):

@@ -15,7 +15,7 @@ LINE = 256
 ROW0 = 48
 POOL_NB = 1696
 PIECES = (0, 256, 384, 512)
-CHUNKS = (0, 384, 896, 1472, 2048)
+CHUNKS = (0, 448, 1024, 1600, 2048)
 
 FLOPS = 2 * D * NQ * N
 

from contextlib import ExitStack

import concourse.mybir as mybir

P = 128
T = 2048
N = 512
D = 512
NQ = 128
PACK = 4
HALF = N // 2
BANK = 2048
CUT = 288
LINE = 256
ROW0 = 48
POOL_NB = 1696
PIECES = (0, 256, 384, 512)
CHUNKS = (0, 448, 1024, 1600, 2048)

FLOPS = 2 * D * NQ * N

F32 = mybir.dt.float32
BF16 = mybir.dt.bfloat16
I32 = mybir.dt.int32
U32 = mybir.dt.uint32
U16 = mybir.dt.uint16
U8 = mybir.dt.uint8
FP8X4 = mybir.dt.float8_e4m3fn_x4
ALU = mybir.AluOpType
ACT = mybir.ActivationFunctionType


def tile_attend_neu_scat_topk_kernel(tc, qT, k_words, k_scales, nb, offs, out):
    nc = tc.nc
    with ExitStack() as ctx:
        sb = ctx.enter_context(tc.tile_pool(name="sb", bufs=1))
        shared = ctx.enter_context(tc.tile_pool(name="shared", bufs=1))
        ps = ctx.enter_context(tc.psum_pool(name="ps", bufs=1))

        offsets = sb.tile([P, N // 16], U16, name="offsets")
        q_raw = sb.tile([P, PACK, NQ], F32, name="q_raw", align_bytes=LINE)
        scale_win = sb.tile([P, T + 4], U8, name="scale_win", align_bytes=LINE)
        word_win = sb.tile([P, T], U32, name="word_win", align_bytes=LINE)
        nb_win = sb.tile([P, T + 1], F32, name="nb_win", align_bytes=LINE)
        ident = sb.tile([P, P], F32, name="ident")
        k_sc = sb.tile([P, N + 4], U8, name="k_sc", align_bytes=64)
        gap = sb.tile([P, P], I32, name="gap")
        win_s = sb.tile([P, T], F32, name="win_s")
        live = P - 1

        def part(lo, hi):
            return offsets[:, lo // 16 : hi // 16]

        nc.gpsimd.iota(gap[:], pattern=[[1, P]], base=0, channel_multiplier=-1)
        nc.scalar.activation(ident[:], gap[:].bitcast(U32), ACT.Relu, bias=1.0, scale=-1.0)
        nc.gpsimd.memset(nb_win[0:live, 0:POOL_NB].bitcast(I32), 0)
        nc.gpsimd.memset(win_s[:].bitcast(I32), 0)
        nc.vector.memset(scale_win[0:ROW0, :].bitcast(I32), 0)
        nc.vector.memset(scale_win[ROW0 + 16 : P, :].bitcast(I32), 0)
        nc.vector.memset(k_sc[:].bitcast(I32), 0)
        nc.vector.memset(nb_win[0:live, POOL_NB : T + 1].bitcast(I32), 0)

        nc.scalar.dma_start(scale_win[ROW0 : ROW0 + 16, 0:T].bitcast(I32), k_scales[0].bitcast(I32))
        nc.sync.dma_start(offsets[:], offs)
        nc.sync.dma_start(nb_win[live:P, 0:T], nb[0:1, :])
        nc.sync.dma_start(q_raw[:], qT[0].rearrange("(p j) w -> p j w", j=PACK))
        nc.sync.dma_start(word_win[:].bitcast(I32), k_words[0].rearrange("p n t -> p (n t)").bitcast(I32))

        halves = [slice(0, HALF), slice(HALF, N)]
        picked = sb.tile([P, N], U8, name="picked", align_bytes=64)

        def lay(a, cols):
            nc.sync.dma_start(
                k_sc[32 * a : 32 * a + 4, cols].bitcast(I32),
                picked[ROW0 + 4 * a : ROW0 + 4 * a + 4, cols].bitcast(I32),
            )

        nc.vector.tensor_copy(picked[:, halves[0]], scale_win[:, 0:T].indirect(part(0, HALF)))
        for a in range(3):
            lay(a, halves[0])
        nc.vector.tensor_copy(picked[:, halves[1]], scale_win[:, 0:T].indirect(part(HALF, N)))
        lay(3, slice(0, N))
        for a in range(3):
            lay(a, halves[1])

        nb_row = sb.tile([P, N], F32, name="nb_row")
        nc.scalar.activation(nb_row[:, halves[0]], nb_win[:, 0:T].indirect(part(0, HALF)), ACT.Copy)
        nc.scalar.activation(nb_row[:, halves[1]], nb_win[:, 0:T].indirect(part(HALF, N)), ACT.Copy)

        q_bf = shared.tile([P, NQ, PACK], BF16, name="q_bf", offset=4 * T - 512, align_bytes=64)
        for rows in (slice(0, 63), slice(63, NQ)):
            nc.vector.tensor_copy(q_bf[:, rows, :], q_raw[:, :, rows].rearrange("p j w -> p w j"))
        q_codes = sb.tile([P, NQ], U32, name="q_codes", align_bytes=64)
        q_sc = sb.tile([P, NQ], U8, name="q_sc", align_bytes=64)
        nc.vector.quantize_mx(out=q_codes[:].bitcast(FP8X4), scales=q_sc[:], in_=q_bf[:].rearrange("p w j -> p (w j)"))

        win_v = shared.tile([P, T], F32, name="win_v", offset=0, align_bytes=64)
        nc.gpsimd.memset(win_v[:].bitcast(I32), 0)

        bias = sb.tile([P, N], F32, name="bias")
        nb_col = []
        for h in range(2):
            turned = ps.tile([P, (4, 16)[h], P], F32, name=f"turned{h}", offset=h * BANK)
            for c in range(2):
                nc.tensor.transpose(turned[:, c, :], nb_row[:, (2 * h + c) * P : (2 * h + c + 1) * P], ident[:])
            col = sb.tile([P, 2], F32, name=f"nb_col{h}")
            nc.scalar.copy(col[:], turned[:, 0:2, live])
            nb_col.append(col)
        for h in range(2):
            spread = ps.tile([P, 2, P], F32, name=f"spread{h}", offset=(5 + h) * BANK)
            for c in range(2):
                nc.tensor.transpose(spread[:, c, :], nb_col[h][:, c : c + 1].to_broadcast([P, P]), ident[:])
            nc.scalar.copy(bias[:, halves[h]], spread[:].rearrange("p c w -> p (c w)"))

        k_codes = shared.tile([P, N], U32, name="k_codes", offset=4 * T, align_bytes=64)
        acc = []
        pieces = [slice(lo, hi) for lo, hi in zip(PIECES, PIECES[1:])]
        for h, cols in enumerate(pieces):
            nc.vector.tensor_copy(k_codes[:, cols], word_win[:].indirect(part(cols.start, cols.stop)))
            a = ps.tile([P, cols.stop - cols.start], F32, name=f"acc{h}", offset=(2 + h) * BANK)
            nc.tensor.matmul_mx(
                out=a[:],
                lhsT=q_codes[:].bitcast(FP8X4),
                lhsT_scale=q_sc[:],
                rhs=k_codes[:, cols].bitcast(FP8X4),
                rhs_scale=k_sc[:, cols],
                start=True,
                stop=True,
            )
            acc.append(a)

        sums = sb.tile([P, N], F32, name="sums")
        extra = CUT - HALF
        nc.vector.tensor_tensor(sums[:, pieces[0]], acc[0][:], bias[:, pieces[0]], ALU.add)
        nc.vector.tensor_tensor(sums[:, HALF:CUT], acc[1][:, 0:extra], bias[:, HALF:CUT], ALU.add)
        nc.vector.tensor_copy(sums[:, CUT : PIECES[2]], acc[1][:, extra:P])
        nc.scalar.copy(sums[:, pieces[2]], acc[2][:])
        nc.scalar.activation(win_s[:].indirect(part(0, CUT)), sums[:, 0:CUT], ACT.Copy)
        nc.vector.tensor_tensor(win_v[:].indirect(part(CUT, N)), sums[:, CUT:N], bias[:, CUT:N], ALU.add)

        result = sb.tile([P, T], F32, name="result", align_bytes=LINE)
        for lo, hi in zip(CHUNKS, CHUNKS[1:]):
            cols = slice(lo, hi)
            nc.vector.tensor_tensor(result[:, cols], win_v[:, cols], win_s[:, cols], ALU.max)
            nc.sync.dma_start(out[0][:, cols], result[:, cols])
